import numpy as np
import ml_dtypes


def mxq(x, axis, fmt="e4m3"):
    dtype, down = {"e4m3": (ml_dtypes.float8_e4m3fn, 7), "e5m2": (ml_dtypes.float8_e5m2, 14)}[fmt]
    v = np.moveaxis(np.asarray(x, np.float32).astype(ml_dtypes.bfloat16).astype(np.float64), axis, -1)
    blocks = v.reshape(v.shape[:-1] + (-1, 32))
    amax = np.abs(blocks).max(-1, keepdims=True)
    byte = np.maximum(np.where(amax > 0, np.frexp(amax)[1] - 1 + 127, 0) - down, 1)
    scale = np.exp2(byte - 127.0)
    codes = (blocks / scale).astype(np.float32).astype(dtype).astype(np.float64)
    return np.moveaxis((codes * scale).reshape(v.shape), -1, axis)


WIDE = False


def mx_kscale(k):
    if not WIDE:
        return np.ones(k)
    levels = np.array([24, -24, 12, -12, 0])
    if k % 512:
        return np.exp2(np.random.permutation(np.resize(levels, k // 32))).repeat(32)
    a = np.empty((k // 512, 16))
    for p in range(k // 512):
        a[p, :8] = np.random.permutation(np.resize(levels, 8))
        for g in range(8):
            far = levels[np.abs(levels - a[p, g]) >= 10]
            a[p, g + 8] = far[np.random.randint(len(far))]
    return np.exp2(a.ravel()).repeat(32)


def f64(x):
    return np.asarray(x).astype(np.float64)


def striped8(idx):
    return np.concatenate([v.reshape(-1, 16).T for v in idx]).astype(np.uint16)


def unstriped8(offs):
    return np.stack([offs[16 * g:16 * g + 16].T.reshape(-1) for g in range(8)]).astype(np.int64)


E2M1 = np.array([0.0, 0.5, 1.0, 1.5, 2.0, 3.0, 4.0, 6.0, -0.0, -0.5, -1.0, -1.5, -2.0, -3.0, -4.0, -6.0])


def pack_weight(w, fmt):
    k, n = w.shape
    w = f64(np.asarray(w, np.float32).astype(ml_dtypes.bfloat16)).reshape(k // 32, 32, n)
    amax = np.abs(w).max(1)
    if fmt == "e4m3":
        byte = np.frexp(amax)[1] - 1 + 127 - 7
    else:
        mant, ex = np.frexp(amax / 6.0)
        byte = np.where(mant > 0.5, ex, ex - 1) + 127
    byte = np.clip(np.where(amax > 0, byte, 1), 1, 254)
    scaled = (w * np.exp2(127.0 - byte)[:, None, :]).reshape(k, n).astype(np.float32)
    by_word = np.ascontiguousarray(scaled.reshape(k // 512, 128, 4, n).transpose(0, 1, 3, 2))
    if fmt == "e4m3":
        words = by_word.astype(ml_dtypes.float8_e4m3fn).view(np.uint8)
    else:
        c = by_word.astype(ml_dtypes.float4_e2m1fn).view(np.uint8) & 0xF
        words = (c[..., 0::2] | (c[..., 1::2] << 4)).reshape(k // 512, 128, 2 * n)
    return np.ascontiguousarray(words), np.ascontiguousarray(byte.astype(np.uint8).reshape(k // 512, 16, n))


def unpack_weight(words, scales, fmt):
    g, _, n = scales.shape
    words = np.ascontiguousarray(words).reshape(g, 128, n, -1)
    if fmt == "e4m3":
        vals = words.view(ml_dtypes.float8_e4m3fn).astype(np.float64)
    else:
        nib = np.empty((g, 128, n, 4), np.uint8)
        nib[..., 0::2] = words & 0xF
        nib[..., 1::2] = words >> 4
        vals = E2M1[nib]
    vals = vals * np.repeat(np.exp2(scales.astype(np.float64) - 127.0), 8, axis=1)[..., None]
    return vals.transpose(0, 1, 3, 2).reshape(g * 512, n)


def planes(y):
    n, m = y.shape
    v = y.astype(np.float32).astype(ml_dtypes.bfloat16).astype(np.float64).reshape(n // 32, 32, m)
    top = np.abs(v).max(1)
    byte = np.clip(np.where(top > 0, np.frexp(top)[1] - 1 + 127 - 7, 1), 1, 254)
    codes = (v * np.exp2(127.0 - byte)[:, None, :]).reshape(n, m).astype(np.float32).astype(ml_dtypes.float8_e4m3fn).view(np.uint8)
    words = codes.reshape(n // 512, 128, 4, m).transpose(0, 1, 3, 2)
    return np.ascontiguousarray(words), np.ascontiguousarray(byte.astype(np.uint8).reshape(n // 512, 16, m))


K, N, T, J = 512, 512, 2048, 1024


def setup_inputs():
    n = np.random.standard_normal
    s = mx_kscale(K)[:, None]
    p_wk = pack_weight(n((K, N)) / np.sqrt(K) / s, "e4m3")
    p_wv = pack_weight(n((K, N)) / np.sqrt(K) / s, "e2m1")
    return {
        "xT": (n((K, T)) * s).astype(np.float32),
        "wgt": np.repeat(np.random.uniform(0.5, 2.0, (8, J)), 16, axis=0).astype(np.float32),
        "wk_words": p_wk[0],
        "wk_scales": p_wk[1],
        "wv_words": p_wv[0],
        "wv_scales": p_wv[1],
        "st": (n((N, J))).astype(np.float32),
        "offs": striped8(np.stack([np.random.permutation(T)[:J] for _ in range(8)])),
    }


def reference(xT, wgt, wk_words, wk_scales, wv_words, wv_scales, st, offs):
    idx = unstriped8(offs)
    rows = np.arange(K)
    xg = f64(wgt)[rows // 4 % 128] * f64(xT)[rows[:, None], idx[rows % 512 // 64]]
    xT_ = mxq(xg, 0, "e4m3")
    wk_ = unpack_weight(wk_words, wk_scales, "e4m3")
    wv_ = unpack_weight(wv_words, wv_scales, "e2m1")
    ke = wk_.T @ xT_
    ve = wv_.T @ xT_
    gate = np.tanh(ke * f64(st))
    out_0 = gate * ve
    return (out_0,) + planes(out_0)

@@ -1,0 +1,195 @@
+from contextlib import ExitStack
+
+import concourse.mybir as mybir
+
+K, N, T, J = 512, 512, 2048, 1024
+FLOPS = 2 * 2 * K * N * J
+
+F32 = mybir.dt.float32
+BF16 = mybir.dt.bfloat16
+I32 = mybir.dt.int32
+U16 = mybir.dt.uint16
+U8 = mybir.dt.uint8
+FP8X4 = mybir.dt.float8_e4m3fn_x4
+FP4X4 = mybir.dt.float4_e2m1fn_x4
+MULT = mybir.AluOpType.mult
+TANH = mybir.ActivationFunctionType.Tanh
+
+P = 128
+PACK = 4
+CHUNK = 256
+UNIT = 128
+CHUNKS = J // CHUNK
+UNITS = J // UNIT
+HALF = J // 2
+
+
+def tile_list_tanhP_kernel(
+    tc, xT, wgt, wk_words, wk_scales, wv_words, wv_scales, st, offs, out_0, out_1, out_2
+):
+    nc = tc.nc
+    with ExitStack() as ctx:
+        keep = ctx.enter_context(tc.tile_pool(name="keep", bufs=1))
+        ring = ctx.enter_context(tc.tile_pool(name="ring", bufs=3))
+        psum = ctx.enter_context(tc.psum_pool(name="psum", bufs=4))
+
+        offsets = keep.tile([P, J // 16], U16, name="offsets")
+        wk_raw = keep.tile([P, N], I32, name="wk_raw")
+        wv_raw = keep.tile([P, 2 * N], U8, name="wv_raw")
+        ws_raw = keep.tile([P, N], U8, name="ws_raw")
+        warm = keep.tile([P, 8], F32, name="warm")
+        warm2 = keep.tile([P, 8], F32, name="warm2")
+
+        nc.gpsimd.memset(ws_raw[:].bitcast(I32), 0)
+        nc.vector.memset(warm[:], 0.0)
+        nc.sync.dma_start(offsets[:], offs)
+        nc.scalar.activation(warm2[:], warm[:], TANH)
+
+        x_rows = xT.rearrange("(p t) c -> p t c", t=PACK)
+        planes = [keep.tile([P, T], F32, name=f"plane{t}") for t in range(PACK)]
+        weight = keep.tile([P, J], F32, name="weight")
+        nc.sync.dma_start(planes[0][:], x_rows[:, 0, :])
+        nc.sync.dma_start(weight[:, :CHUNK], wgt[:, :CHUNK])
+        nc.sync.dma_start(weight[:, CHUNK:], wgt[:, CHUNK:])
+        nc.sync.dma_start(wk_raw[:], wk_words[0].rearrange("p n i -> p (n i)").bitcast(I32))
+        nc.sync.dma_start(wv_raw[:].bitcast(I32), wv_words[0].bitcast(I32))
+
+        def load_scales(q):
+            nc.sync.dma_start(
+                ws_raw[32 * q : 32 * q + 4, :].bitcast(I32), wv_scales[0, 4 * q : 4 * q + 4, :].bitcast(I32)
+            )
+            nc.sync.dma_start(
+                ws_raw[32 * q + 4 : 32 * q + 8, :].bitcast(I32), wk_scales[0, 4 * q : 4 * q + 4, :].bitcast(I32)
+            )
+
+        load_scales(0)
+        nc.sync.dma_start(planes[1][:], x_rows[:, 1, :])
+        for q in range(1, 4):
+            load_scales(q)
+        for t in range(2, PACK):
+            nc.sync.dma_start(planes[t][:], x_rows[:, t, :])
+        st_rows = st.rearrange("(p t) j -> p t j", t=PACK)
+        state = [keep.tile([P, PACK, CHUNK], F32, name=f"state{c}") for c in range(CHUNKS)]
+        for c in range(CHUNKS):
+            nc.sync.dma_start(state[c][:], st_rows[:, :, c * CHUNK : (c + 1) * CHUNK])
+
+        wk = keep.tile([P, PACK, P], I32, name="wk", align_bytes=64)
+        wv = keep.tile([P, PACK, P], U16, name="wv", align_bytes=64)
+        ws = keep.tile([P, PACK, P], U8, name="ws", align_bytes=64)
+
+        def deal(dealt, raw):
+            nc.vector.tensor_copy(dealt.rearrange("p t m -> p m t"), raw.rearrange("p (m t) -> p m t", t=PACK))
+
+        low = keep.tile([P, 2, J], F32, name="low")
+        high = [keep.tile([P, 2, CHUNK], F32, name=f"high{c}") for c in range(CHUNKS)]
+        xg = [keep.tile([P, CHUNK, PACK], BF16, name=f"xg{c}", align_bytes=64) for c in range(CHUNKS)]
+        x_codes = [keep.tile([P, CHUNK], I32, name=f"x_codes{c}", align_bytes=64) for c in range(CHUNKS)]
+        x_scales = [keep.tile([P, CHUNK], U8, name=f"x_scales{c}", align_bytes=64) for c in range(CHUNKS)]
+        y = [keep.tile([P, PACK, CHUNK], F32, name=f"y{c}") for c in range(CHUNKS)]
+        y_codes = keep.tile([P, J], I32, name="y_codes", align_bytes=64)
+        y_scales = keep.tile([P, J], U8, name="y_scales", align_bytes=64)
+
+        def gather(out, t, j0, j1):
+            nc.vector.tensor_tensor(out, planes[t][:].indirect(offsets[:, j0 // 16 : j1 // 16]), weight[:, j0:j1], MULT)
+
+        def gather_high(t, c):
+            gather(high[c][:, t - 2, :], t, c * CHUNK, (c + 1) * CHUNK)
+
+        def weave_low(c):
+            nc.scalar.copy(xg[c][:, :, 0:2], low[:, :, c * CHUNK : (c + 1) * CHUNK].rearrange("p t j -> p j t"))
+
+        def weave_high(c):
+            nc.scalar.copy(xg[c][:, :, 2:4], high[c][:].rearrange("p t j -> p j t"))
+
+        def quantize_x(c):
+            nc.vector.quantize_mx(
+                out=x_codes[c][:].bitcast(FP8X4), scales=x_scales[c][:], in_=xg[c][:].rearrange("p j t -> p (j t)")
+            )
+
+        ke, ve, gate = {}, {}, {}
+        woven = [keep.tile([P, CHUNK, PACK], BF16, name=f"woven{c}", align_bytes=64) for c in range(CHUNKS)]
+
+        def place(u):
+            c, j0 = divmod(u * UNIT, CHUNK)
+            return c, slice(j0, j0 + UNIT)
+
+        def multiply(u):
+            c, cols = place(u)
+            ke[u] = psum.tile([P, PACK, UNIT], F32, name="ke")
+            ve[u] = psum.tile([P, PACK, UNIT], F32, name="ve")
+            for t in range(PACK):
+                nc.tensor.matmul_mx(
+                    out=ke[u][:, t, :], lhsT=wk[:, t, :].bitcast(FP8X4), lhsT_scale=ws[4:P, t, :],
+                    rhs=x_codes[c][:, cols].bitcast(FP8X4), rhs_scale=x_scales[c][:, cols], start=True, stop=True,
+                )
+            for t in range(PACK):
+                nc.tensor.matmul_mx(
+                    out=ve[u][:, t, :], lhsT=wv[:, t, :].bitcast(FP4X4),
+                    lhsT_scale=ws[:, t, :],
+                    rhs=x_codes[c][:, cols].bitcast(FP8X4), rhs_scale=x_scales[c][:, cols], start=True, stop=True,
+                )
+
+        def open_gate(u):
+            c, cols = place(u)
+            logit = ring.tile([P, PACK, UNIT], F32, name="logit")
+            gate[u] = ring.tile([P, PACK, UNIT], F32, name="gate")
+            nc.vector.tensor_tensor(logit[:], ke[u][:], state[c][:, :, cols], MULT)
+            nc.scalar.activation(gate[u][:], logit[:], TANH)
+
+        def let_through(u):
+            c, cols = place(u)
+            nc.vector.tensor_tensor(y[c][:, :, cols], ve[u][:], gate[u][:], MULT)
+            weave = nc.vector.tensor_copy if u == UNITS - 1 else nc.scalar.copy
+            weave(
+                woven[c][:, cols, :].rearrange("p (a i) t -> p a t i", i=4),
+                y[c][:, :, cols].rearrange("p t (a i) -> p a t i", i=4),
+            )
+            if c == CHUNKS - 1:
+                nc.sync.dma_start(out_rows[:, :, u * UNIT : (u + 1) * UNIT], y[c][:, :, cols])
+            elif cols.stop == CHUNK:
+                nc.sync.dma_start(out_rows[:, :, c * CHUNK : (c + 1) * CHUNK], y[c][:])
+
+        def quantize_y(u):
+            c, cols = place(u)
+            if c < CHUNKS - 1:
+                if cols.stop < CHUNK:
+                    return
+                cols = slice(0, CHUNK)
+            js = slice(c * CHUNK + cols.start, c * CHUNK + cols.stop)
+            nc.vector.quantize_mx(
+                out=y_codes[:, js].bitcast(FP8X4), scales=y_scales[:, js],
+                in_=woven[c][:, cols, :].rearrange("p j t -> p (j t)"),
+            )
+            nc.sync.dma_start(out_words[:, js], y_codes[:, js])
+
+        out_rows = out_0.rearrange("(p t) j -> p t j", t=PACK)
+        out_words = out_1[0].rearrange("p j i -> p (j i)").bitcast(I32)
+
+        gather(low[:, 0, :CHUNK], 0, 0, CHUNK)
+        gather(low[:, 0, CHUNK:], 0, CHUNK, J)
+        deal(wk[:], wk_raw[:])
+        deal(wv[:], wv_raw[:].bitcast(U16))
+        gather(low[:, 1, :], 1, 0, J)
+        deal(ws[:], ws_raw[:])
+        for c in range(CHUNKS):
+            weave_low(c)
+            gather_high(2, c)
+        for c in range(CHUNKS + 1):
+            if c < CHUNKS:
+                gather_high(3, c)
+                weave_high(c)
+            if c > 0:
+                quantize_x(c - 1)
+        for s in range(UNITS + 2):
+            if s < UNITS:
+                multiply(s)
+                open_gate(s)
+            if 1 <= s <= UNITS:
+                let_through(s - 1)
+            if s >= 2:
+                quantize_y(s - 2)
+        for q in range(4):
+            queue = nc.scalar if q % 2 else nc.sync
+            queue.dma_start(
+                out_2[0, 4 * q : 4 * q + 4, :].bitcast(I32), y_scales[32 * q : 32 * q + 4, :].bitcast(I32)
+            )

@@ -13,6 +13,7 @@ U8 = mybir.dt.uint8
 FP8X4 = mybir.dt.float8_e4m3fn_x4
 FP4X4 = mybir.dt.float4_e2m1fn_x4
 MULT = mybir.AluOpType.mult
+ADD = mybir.AluOpType.add
 TANH = mybir.ActivationFunctionType.Tanh
 
 P = 128
@@ -21,7 +22,8 @@ CHUNK = 256
 UNIT = 128
 CHUNKS = J // CHUNK
 UNITS = J // UNIT
-HALF = J // 2
+POOL_PRODUCT = (3, 5)
+POOL_WEAVE = (0, 2, 4)
 
 
 def tile_list_tanhP_kernel(
@@ -37,13 +39,9 @@ def tile_list_tanhP_kernel(
         wk_raw = keep.tile([P, N], I32, name="wk_raw")
         wv_raw = keep.tile([P, 2 * N], U8, name="wv_raw")
         ws_raw = keep.tile([P, N], U8, name="ws_raw")
-        warm = keep.tile([P, 8], F32, name="warm")
-        warm2 = keep.tile([P, 8], F32, name="warm2")
 
         nc.gpsimd.memset(ws_raw[:].bitcast(I32), 0)
-        nc.vector.memset(warm[:], 0.0)
         nc.sync.dma_start(offsets[:], offs)
-        nc.scalar.activation(warm2[:], warm[:], TANH)
 
         x_rows = xT.rearrange("(p t) c -> p t c", t=PACK)
         planes = [keep.tile([P, T], F32, name=f"plane{t}") for t in range(PACK)]
@@ -133,34 +131,61 @@ def tile_list_tanhP_kernel(
             c, cols = place(u)
             logit = ring.tile([P, PACK, UNIT], F32, name="logit")
             gate[u] = ring.tile([P, PACK, UNIT], F32, name="gate")
+            if u in POOL_PRODUCT:
+                held = ring.tile([P, PACK, UNIT], F32, name="held")
+                nc.scalar.copy(held[:], ve[u][:])
+                ve[u] = held
             nc.vector.tensor_tensor(logit[:], ke[u][:], state[c][:, :, cols], MULT)
             nc.scalar.activation(gate[u][:], logit[:], TANH)
 
-        def let_through(u):
-            c, cols = place(u)
-            nc.vector.tensor_tensor(y[c][:, :, cols], ve[u][:], gate[u][:], MULT)
-            weave = nc.vector.tensor_copy if u == UNITS - 1 else nc.scalar.copy
-            weave(
-                woven[c][:, cols, :].rearrange("p (a i) t -> p a t i", i=4),
-                y[c][:, :, cols].rearrange("p t (a i) -> p a t i", i=4),
-            )
-            if c == CHUNKS - 1:
-                nc.sync.dma_start(out_rows[:, :, u * UNIT : (u + 1) * UNIT], y[c][:, :, cols])
-            elif cols.stop == CHUNK:
-                nc.sync.dma_start(out_rows[:, :, c * CHUNK : (c + 1) * CHUNK], y[c][:])
+        def weave_y(engine, c, cols):
+            out = woven[c][:, cols, :].rearrange("p (a i) t -> p a t i", i=4)
+            src = y[c][:, :, cols].rearrange("p t (a i) -> p a t i", i=4)
+            if engine == "pool":
+                nc.gpsimd.tensor_scalar(out, src, 1.0, -0.0, MULT, ADD)
+            elif engine == "act":
+                nc.scalar.copy(out, src)
+            else:
+                nc.vector.tensor_copy(out, src)
 
-        def quantize_y(u):
-            c, cols = place(u)
-            if c < CHUNKS - 1:
-                if cols.stop < CHUNK:
-                    return
-                cols = slice(0, CHUNK)
+        def quantize_cols(c, cols):
             js = slice(c * CHUNK + cols.start, c * CHUNK + cols.stop)
             nc.vector.quantize_mx(
                 out=y_codes[:, js].bitcast(FP8X4), scales=y_scales[:, js],
                 in_=woven[c][:, cols, :].rearrange("p j t -> p (j t)"),
             )
+
+        def let_through(u):
+            c, cols = place(u)
+            if u in POOL_PRODUCT:
+                nc.gpsimd.tensor_tensor(y[c][:, :, cols], ve[u][:], gate[u][:], MULT)
+            else:
+                nc.vector.tensor_tensor(y[c][:, :, cols], ve[u][:], gate[u][:], MULT)
+            weave_y("pool" if u in POOL_WEAVE else "act", c, cols)
+            if c == CHUNKS - 1:
+                nc.sync.dma_start(out_rows[:, :, u * UNIT : (u + 1) * UNIT], y[c][:, :, cols])
+            elif cols.stop == CHUNK:
+                nc.sync.dma_start(out_rows[:, :, c * CHUNK : (c + 1) * CHUNK], y[c][:])
+
+        def quantize_y(c):
+            quantize_cols(c, slice(0, CHUNK))
+            js = slice(c * CHUNK, (c + 1) * CHUNK)
             nc.sync.dma_start(out_words[:, js], y_codes[:, js])
+
+        def finish():
+            u = UNITS - 1
+            c, cols = place(u)
+            halves = [slice(0, UNIT // 2), slice(UNIT // 2, UNIT)]
+            placed = [slice(cols.start + h.start, cols.start + h.stop) for h in halves]
+            for h, at in zip(halves, placed):
+                nc.vector.tensor_tensor(y[c][:, :, at], ve[u][:, :, h], gate[u][:, :, h], MULT)
+            weave_y("act", c, placed[0])
+            nc.sync.dma_start(out_rows[:, :, u * UNIT :], y[c][:, :, cols])
+            quantize_cols(c, slice(0, UNIT))
+            weave_y("vector", c, placed[1])
+            for at in placed:
+                quantize_cols(c, at)
+            nc.sync.dma_start(out_words[:, c * CHUNK :], y_codes[:, c * CHUNK :])
 
         out_rows = out_0.rearrange("(p t) j -> p t j", t=PACK)
         out_words = out_1[0].rearrange("p j i -> p (j i)").bitcast(I32)
@@ -180,14 +205,14 @@ def tile_list_tanhP_kernel(
                 weave_high(c)
             if c > 0:
                 quantize_x(c - 1)
-        for s in range(UNITS + 2):
-            if s < UNITS:
-                multiply(s)
-                open_gate(s)
-            if 1 <= s <= UNITS:
+        for s in range(UNITS):
+            multiply(s)
+            open_gate(s)
+            if s >= 1:
                 let_through(s - 1)
-            if s >= 2:
-                quantize_y(s - 2)
+            if s >= 3 and s % 2:
+                quantize_y((s - 3) // 2)
+        finish()
         for q in range(4):
             queue = nc.scalar if q % 2 else nc.sync
             queue.dma_start(

@@ -22,8 +22,8 @@ CHUNK = 256
 UNIT = 128
 CHUNKS = J // CHUNK
 UNITS = J // UNIT
-POOL_PRODUCT = (3, 5)
-POOL_WEAVE = (0, 2, 4)
+POOL_PRODUCT = ()
+POOL_WEAVE = ()
 
 
 def tile_list_tanhP_kernel(
@@ -32,8 +32,9 @@ def tile_list_tanhP_kernel(
     nc = tc.nc
     with ExitStack() as ctx:
         keep = ctx.enter_context(tc.tile_pool(name="keep", bufs=1))
-        ring = ctx.enter_context(tc.tile_pool(name="ring", bufs=3))
-        psum = ctx.enter_context(tc.psum_pool(name="psum", bufs=4))
+        ring = ctx.enter_context(tc.tile_pool(name="ring", bufs=4))
+        key_banks = ctx.enter_context(tc.psum_pool(name="key_banks", bufs=3))
+        value_banks = ctx.enter_context(tc.psum_pool(name="value_banks", bufs=5))
 
         offsets = keep.tile([P, J // 16], U16, name="offsets")
         wk_raw = keep.tile([P, N], I32, name="wk_raw")
@@ -49,23 +50,21 @@ def tile_list_tanhP_kernel(
         nc.sync.dma_start(planes[0][:], x_rows[:, 0, :])
         nc.sync.dma_start(weight[:, :CHUNK], wgt[:, :CHUNK])
         nc.sync.dma_start(weight[:, CHUNK:], wgt[:, CHUNK:])
-        nc.sync.dma_start(wk_raw[:], wk_words[0].rearrange("p n i -> p (n i)").bitcast(I32))
         nc.sync.dma_start(wv_raw[:].bitcast(I32), wv_words[0].bitcast(I32))
+        nc.sync.dma_start(planes[1][:], x_rows[:, 1, :])
+        nc.sync.dma_start(wk_raw[:], wk_words[0].rearrange("p n i -> p (n i)").bitcast(I32))
 
         def load_scales(q):
-            nc.sync.dma_start(
-                ws_raw[32 * q : 32 * q + 4, :].bitcast(I32), wv_scales[0, 4 * q : 4 * q + 4, :].bitcast(I32)
-            )
-            nc.sync.dma_start(
-                ws_raw[32 * q + 4 : 32 * q + 8, :].bitcast(I32), wk_scales[0, 4 * q : 4 * q + 4, :].bitcast(I32)
-            )
+            for first, rows in ((0, wv_scales), (4, wk_scales)):
+                at = 32 * q + first
+                nc.sync.dma_start(ws_raw[at : at + 4, :].bitcast(I32), rows[0, 4 * q : 4 * q + 4, :].bitcast(I32))
 
         load_scales(0)
-        nc.sync.dma_start(planes[1][:], x_rows[:, 1, :])
-        for q in range(1, 4):
-            load_scales(q)
-        for t in range(2, PACK):
-            nc.sync.dma_start(planes[t][:], x_rows[:, t, :])
+        load_scales(1)
+        nc.sync.dma_start(planes[2][:], x_rows[:, 2, :])
+        load_scales(2)
+        load_scales(3)
+        nc.sync.dma_start(planes[3][:], x_rows[:, 3, :])
         st_rows = st.rearrange("(p t) j -> p t j", t=PACK)
         state = [keep.tile([P, PACK, CHUNK], F32, name=f"state{c}") for c in range(CHUNKS)]
         for c in range(CHUNKS):
@@ -79,7 +78,7 @@ def tile_list_tanhP_kernel(
             nc.vector.tensor_copy(dealt.rearrange("p t m -> p m t"), raw.rearrange("p (m t) -> p m t", t=PACK))
 
         low = keep.tile([P, 2, J], F32, name="low")
-        high = [keep.tile([P, 2, CHUNK], F32, name=f"high{c}") for c in range(CHUNKS)]
+        high = [keep.tile([P, 2, CHUNK], F32, name=f"high{c}") for c in range(CHUNKS - 1)]
         xg = [keep.tile([P, CHUNK, PACK], BF16, name=f"xg{c}", align_bytes=64) for c in range(CHUNKS)]
         x_codes = [keep.tile([P, CHUNK], I32, name=f"x_codes{c}", align_bytes=64) for c in range(CHUNKS)]
         x_scales = [keep.tile([P, CHUNK], U8, name=f"x_scales{c}", align_bytes=64) for c in range(CHUNKS)]
@@ -113,8 +112,8 @@ def tile_list_tanhP_kernel(
 
         def multiply(u):
             c, cols = place(u)
-            ke[u] = psum.tile([P, PACK, UNIT], F32, name="ke")
-            ve[u] = psum.tile([P, PACK, UNIT], F32, name="ve")
+            ke[u] = key_banks.tile([P, PACK, UNIT], F32, name="ke")
+            ve[u] = value_banks.tile([P, PACK, UNIT], F32, name="ve")
             for t in range(PACK):
                 nc.tensor.matmul_mx(
                     out=ke[u][:, t, :], lhsT=wk[:, t, :].bitcast(FP8X4), lhsT_scale=ws[4:P, t, :],
@@ -162,7 +161,7 @@ def tile_list_tanhP_kernel(
             else:
                 nc.vector.tensor_tensor(y[c][:, :, cols], ve[u][:], gate[u][:], MULT)
             weave_y("pool" if u in POOL_WEAVE else "act", c, cols)
-            if c == CHUNKS - 1:
+            if c >= CHUNKS - 2:
                 nc.sync.dma_start(out_rows[:, :, u * UNIT : (u + 1) * UNIT], y[c][:, :, cols])
             elif cols.stop == CHUNK:
                 nc.sync.dma_start(out_rows[:, :, c * CHUNK : (c + 1) * CHUNK], y[c][:])
@@ -192,26 +191,35 @@ def tile_list_tanhP_kernel(
 
         gather(low[:, 0, :CHUNK], 0, 0, CHUNK)
         gather(low[:, 0, CHUNK:], 0, CHUNK, J)
-        deal(wk[:], wk_raw[:])
         deal(wv[:], wv_raw[:].bitcast(U16))
         gather(low[:, 1, :], 1, 0, J)
-        deal(ws[:], ws_raw[:])
+        deal(wk[:], wk_raw[:])
         for c in range(CHUNKS):
             weave_low(c)
+        for c in range(CHUNKS - 1):
             gather_high(2, c)
-        for c in range(CHUNKS + 1):
-            if c < CHUNKS:
-                gather_high(3, c)
-                weave_high(c)
-            if c > 0:
-                quantize_x(c - 1)
+        deal(ws[:], ws_raw[:])
+        for c in range(CHUNKS - 1):
+            gather_high(3, c)
+            weave_high(c)
+        quantize_x(0)
+        high.append(keep.tile([P, 2, CHUNK], F32, name="high_last", tag="xg0", align_bytes=64))
+        gather_high(2, CHUNKS - 1)
+        gather_high(3, CHUNKS - 1)
+        weave_high(CHUNKS - 1)
+        quantize_x(1)
+        quantize_x(2)
         for s in range(UNITS):
             multiply(s)
             open_gate(s)
-            if s >= 1:
-                let_through(s - 1)
-            if s >= 3 and s % 2:
-                quantize_y((s - 3) // 2)
+            if s == 0:
+                quantize_x(CHUNKS - 1)
+            if s >= 2:
+                let_through(s - 2)
+            if s >= 4 and s % 2 == 0:
+                quantize_y((s - 4) // 2)
+        let_through(UNITS - 2)
+        quantize_y(CHUNKS - 2)
         finish()
         for q in range(4):
             queue = nc.scalar if q % 2 else nc.sync

@@ -22,8 +22,8 @@ CHUNK = 256
 UNIT = 128
 CHUNKS = J // CHUNK
 UNITS = J // UNIT
-POOL_PRODUCT = ()
-POOL_WEAVE = ()
+POOL_PRODUCT = (0,)
+POOL_WEAVE = (0, 1)
 
 
 def tile_list_tanhP_kernel(
@@ -104,7 +104,10 @@ def tile_list_tanhP_kernel(
             )
 
         ke, ve, gate = {}, {}, {}
-        woven = [keep.tile([P, CHUNK, PACK], BF16, name=f"woven{c}", align_bytes=64) for c in range(CHUNKS)]
+        first = keep.tile([P, 2 * CHUNK, PACK], BF16, name="woven_first", align_bytes=64)
+        woven = {0: first[:, :CHUNK, :], 1: first[:, CHUNK:, :]}
+        woven[2] = keep.tile([P, CHUNK, PACK], BF16, name="woven_third", align_bytes=64)
+        woven[3] = keep.tile([P, CHUNK, PACK], BF16, name="woven_last", align_bytes=64)
 
         def place(u):
             c, j0 = divmod(u * UNIT, CHUNK)
@@ -137,11 +140,14 @@ def tile_list_tanhP_kernel(
             nc.vector.tensor_tensor(logit[:], ke[u][:], state[c][:, :, cols], MULT)
             nc.scalar.activation(gate[u][:], logit[:], TANH)
 
+        ones = keep.tile([P, PACK, UNIT], F32, name="ones")
+        nc.gpsimd.memset(ones[:], 1.0)
+
         def weave_y(engine, c, cols):
             out = woven[c][:, cols, :].rearrange("p (a i) t -> p a t i", i=4)
             src = y[c][:, :, cols].rearrange("p t (a i) -> p a t i", i=4)
             if engine == "pool":
-                nc.gpsimd.tensor_scalar(out, src, 1.0, -0.0, MULT, ADD)
+                nc.gpsimd.tensor_tensor(out, src, ones[:].rearrange("p t (a i) -> p a t i", i=4), MULT)
             elif engine == "act":
                 nc.scalar.copy(out, src)
             else:
@@ -171,6 +177,13 @@ def tile_list_tanhP_kernel(
             js = slice(c * CHUNK, (c + 1) * CHUNK)
             nc.sync.dma_start(out_words[:, js], y_codes[:, js])
 
+        def quantize_first():
+            js = slice(0, 2 * CHUNK)
+            nc.vector.quantize_mx(
+                out=y_codes[:, js].bitcast(FP8X4), scales=y_scales[:, js], in_=first[:].rearrange("p j t -> p (j t)")
+            )
+            nc.sync.dma_start(out_words[:, js], y_codes[:, js])
+
         def finish():
             u = UNITS - 1
             c, cols = place(u)
@@ -192,7 +205,8 @@ def tile_list_tanhP_kernel(
         gather(low[:, 0, :CHUNK], 0, 0, CHUNK)
         gather(low[:, 0, CHUNK:], 0, CHUNK, J)
         deal(wv[:], wv_raw[:].bitcast(U16))
-        gather(low[:, 1, :], 1, 0, J)
+        gather(low[:, 1, : J // 2], 1, 0, J // 2)
+        gather(low[:, 1, J // 2 :], 1, J // 2, J)
         deal(wk[:], wk_raw[:])
         for c in range(CHUNKS):
             weave_low(c)
@@ -216,8 +230,7 @@ def tile_list_tanhP_kernel(
                 quantize_x(CHUNKS - 1)
             if s >= 2:
                 let_through(s - 2)
-            if s >= 4 and s % 2 == 0:
-                quantize_y((s - 4) // 2)
+        quantize_first()
         let_through(UNITS - 2)
         quantize_y(CHUNKS - 2)
         finish()

@@ -46,10 +46,23 @@ def tile_list_tanhP_kernel(
 
         x_rows = xT.rearrange("(p t) c -> p t c", t=PACK)
         planes = [keep.tile([P, T], F32, name=f"plane{t}") for t in range(PACK)]
-        weight = keep.tile([P, J], F32, name="weight")
+        weight = keep.tile([P, J], F32, name="weight", align_bytes=64)
+        w_rows = keep.tile([P, 64], F32, name="w_rows", align_bytes=64)
+        w_turned = keep.tile([P, 64], F32, name="w_turned", align_bytes=64)
+        w_spread = keep.tile([P, J], F32, name="w_spread", align_bytes=64)
+        nc.sync.dma_start(w_rows[:], wgt[0:P:16, :].rearrange("g (i c) -> g i c", c=64))
         nc.sync.dma_start(planes[0][:], x_rows[:, 0, :])
-        nc.sync.dma_start(weight[:, :CHUNK], wgt[:, :CHUNK])
-        nc.sync.dma_start(weight[:, CHUNK:], wgt[:, CHUNK:])
+        for b in range(2):
+            nc.vector.transpose(w_turned[:, 32 * b : 32 * b + 32], w_rows[:, 32 * b : 32 * b + 32])
+        for half in range(2):
+            js = slice(half * J // 2, (half + 1) * J // 2)
+            nc.vector.tensor_copy(
+                w_spread[:, js].rearrange("p (i b h r) -> p i b h r", b=2, h=2, r=16),
+                w_turned[:].rearrange("p (b h i) -> p i b h", b=2, h=2)[:, 8 * half : 8 * half + 8].unsqueeze(4).to_broadcast([P, 8, 2, 2, 16]),
+            )
+        for half in range(2):
+            js = slice(half * J // 2, (half + 1) * J // 2)
+            nc.vector.transpose(weight[:, js], w_spread[:, js])
         nc.sync.dma_start(wv_raw[:].bitcast(I32), wv_words[0].bitcast(I32))
         nc.sync.dma_start(planes[1][:], x_rows[:, 1, :])
         nc.sync.dma_start(wk_raw[:], wk_words[0].rearrange("p n i -> p (n i)").bitcast(I32))

@@ -39,9 +39,10 @@ def tile_list_tanhP_kernel(
         offsets = keep.tile([P, J // 16], U16, name="offsets")
         wk_raw = keep.tile([P, N], I32, name="wk_raw")
         wv_raw = keep.tile([P, 2 * N], U8, name="wv_raw")
-        ws_raw = keep.tile([P, N], U8, name="ws_raw")
+        all_scales = keep.tile([P, J], U8, name="all_scales", align_bytes=64)
+        ws_raw = all_scales[:, CHUNK // 2 : CHUNK // 2 + N]
 
-        nc.gpsimd.memset(ws_raw[:].bitcast(I32), 0)
+        nc.gpsimd.memset(ws_raw.bitcast(I32), 0)
         nc.sync.dma_start(offsets[:], offs)
 
         x_rows = xT.rearrange("(p t) c -> p t c", t=PACK)
@@ -72,12 +73,11 @@ def tile_list_tanhP_kernel(
                 at = 32 * q + first
                 nc.sync.dma_start(ws_raw[at : at + 4, :].bitcast(I32), rows[0, 4 * q : 4 * q + 4, :].bitcast(I32))
 
-        load_scales(0)
-        load_scales(1)
         nc.sync.dma_start(planes[2][:], x_rows[:, 2, :])
-        load_scales(2)
-        load_scales(3)
+        load_scales(0)
         nc.sync.dma_start(planes[3][:], x_rows[:, 3, :])
+        for q in range(1, 4):
+            load_scales(q)
         st_rows = st.rearrange("(p t) j -> p t j", t=PACK)
         state = [keep.tile([P, PACK, CHUNK], F32, name=f"state{c}") for c in range(CHUNKS)]
         for c in range(CHUNKS):
@@ -91,10 +91,12 @@ def tile_list_tanhP_kernel(
             nc.vector.tensor_copy(dealt.rearrange("p t m -> p m t"), raw.rearrange("p (m t) -> p m t", t=PACK))
 
         low = keep.tile([P, 2, J], F32, name="low")
-        high = [keep.tile([P, 2, CHUNK], F32, name=f"high{c}") for c in range(CHUNKS - 1)]
-        xg = [keep.tile([P, CHUNK, PACK], BF16, name=f"xg{c}", align_bytes=64) for c in range(CHUNKS)]
+        shared = keep.tile([P, 2 * J + CHUNK], F32, name="shared", align_bytes=64)
+        high = shared[:, : 2 * J].rearrange("p (t j) -> p t j", t=2)
+        xg = [shared[:, 2 * J - CHUNK :].bitcast(BF16).rearrange("p (j t) -> p j t", t=PACK)]
+        xg.extend(keep.tile([P, CHUNK, PACK], BF16, name=f"xg{c}", align_bytes=64)[:] for c in range(1, CHUNKS))
         x_codes = [keep.tile([P, CHUNK], I32, name=f"x_codes{c}", align_bytes=64) for c in range(CHUNKS)]
-        x_scales = [keep.tile([P, CHUNK], U8, name=f"x_scales{c}", align_bytes=64) for c in range(CHUNKS)]
+        x_scales = [all_scales[:, c * CHUNK : (c + 1) * CHUNK] for c in range(CHUNKS)]
         y = [keep.tile([P, PACK, CHUNK], F32, name=f"y{c}") for c in range(CHUNKS)]
         y_codes = keep.tile([P, J], I32, name="y_codes", align_bytes=64)
         y_scales = keep.tile([P, J], U8, name="y_scales", align_bytes=64)
@@ -103,17 +105,17 @@ def tile_list_tanhP_kernel(
             nc.vector.tensor_tensor(out, planes[t][:].indirect(offsets[:, j0 // 16 : j1 // 16]), weight[:, j0:j1], MULT)
 
         def gather_high(t, c):
-            gather(high[c][:, t - 2, :], t, c * CHUNK, (c + 1) * CHUNK)
+            gather(high[:, t - 2, c * CHUNK : (c + 1) * CHUNK], t, c * CHUNK, (c + 1) * CHUNK)
 
         def weave_low(c):
             nc.scalar.copy(xg[c][:, :, 0:2], low[:, :, c * CHUNK : (c + 1) * CHUNK].rearrange("p t j -> p j t"))
 
         def weave_high(c):
-            nc.scalar.copy(xg[c][:, :, 2:4], high[c][:].rearrange("p t j -> p j t"))
+            nc.scalar.copy(xg[c][:, :, 2:4], high[:, :, c * CHUNK : (c + 1) * CHUNK].rearrange("p t j -> p j t"))
 
         def quantize_x(c):
             nc.vector.quantize_mx(
-                out=x_codes[c][:].bitcast(FP8X4), scales=x_scales[c][:], in_=xg[c][:].rearrange("p j t -> p (j t)")
+                out=x_codes[c][:].bitcast(FP8X4), scales=x_scales[c], in_=xg[c].rearrange("p j t -> p (j t)")
             )
 
         ke, ve, gate = {}, {}, {}
@@ -215,23 +217,20 @@ def tile_list_tanhP_kernel(
         out_rows = out_0.rearrange("(p t) j -> p t j", t=PACK)
         out_words = out_1[0].rearrange("p j i -> p (j i)").bitcast(I32)
 
-        gather(low[:, 0, :CHUNK], 0, 0, CHUNK)
-        gather(low[:, 0, CHUNK:], 0, CHUNK, J)
+        gather(low[:, 0, : J // 2], 0, 0, J // 2)
+        gather(low[:, 0, J // 2 :], 0, J // 2, J)
         deal(wv[:], wv_raw[:].bitcast(U16))
         gather(low[:, 1, : J // 2], 1, 0, J // 2)
         gather(low[:, 1, J // 2 :], 1, J // 2, J)
         deal(wk[:], wk_raw[:])
         for c in range(CHUNKS):
             weave_low(c)
-        for c in range(CHUNKS - 1):
-            gather_high(2, c)
-        deal(ws[:], ws_raw[:])
+        gather(high[:, 0, :], 2, 0, J)
         for c in range(CHUNKS - 1):
             gather_high(3, c)
             weave_high(c)
+        deal(ws[:], ws_raw)
         quantize_x(0)
-        high.append(keep.tile([P, 2, CHUNK], F32, name="high_last", tag="xg0", align_bytes=64))
-        gather_high(2, CHUNKS - 1)
         gather_high(3, CHUNKS - 1)
         weave_high(CHUNKS - 1)
         quantize_x(1)

@@ -18,12 +18,16 @@ TANH = mybir.ActivationFunctionType.Tanh
 
 P = 128
 PACK = 4
+GROUP = 16
+SQUARE = 32
 CHUNK = 256
-UNIT = 128
 CHUNKS = J // CHUNK
-UNITS = J // UNIT
-POOL_PRODUCT = (0,)
-POOL_WEAVE = (0, 1)
+PAIR = 2
+UNITS = CHUNKS * PACK // PAIR
+HALF = CHUNK // 2
+LAG = 2
+GPSIMD_UNITS = 2
+GPSIMD_CHUNKS = 2
 
 
 def tile_list_tanhP_kernel(
@@ -32,220 +36,192 @@ def tile_list_tanhP_kernel(
     nc = tc.nc
     with ExitStack() as ctx:
         keep = ctx.enter_context(tc.tile_pool(name="keep", bufs=1))
-        ring = ctx.enter_context(tc.tile_pool(name="ring", bufs=4))
+        ring = ctx.enter_context(tc.tile_pool(name="ring", bufs=5))
         key_banks = ctx.enter_context(tc.psum_pool(name="key_banks", bufs=3))
         value_banks = ctx.enter_context(tc.psum_pool(name="value_banks", bufs=5))
 
-        offsets = keep.tile([P, J // 16], U16, name="offsets")
+        def chunk_cols(c):
+            return slice(c * CHUNK, (c + 1) * CHUNK)
+
+        offsets = keep.tile([P, J // GROUP], U16, name="offsets")
+        w_rows = keep.tile([P, J // GROUP], F32, name="w_rows", align_bytes=64)
+        planes = [keep.tile([P, T], F32, name=f"plane{t}") for t in range(PACK)]
         wk_raw = keep.tile([P, N], I32, name="wk_raw")
         wv_raw = keep.tile([P, 2 * N], U8, name="wv_raw")
-        all_scales = keep.tile([P, J], U8, name="all_scales", align_bytes=64)
-        ws_raw = all_scales[:, CHUNK // 2 : CHUNK // 2 + N]
-
-        nc.gpsimd.memset(ws_raw.bitcast(I32), 0)
-        nc.sync.dma_start(offsets[:], offs)
-
+        x_scales = keep.tile([P, J], U8, name="x_scales", align_bytes=64)
+        ws_raw = x_scales[:, HALF : HALF + N]
+        state = [keep.tile([P, PACK, CHUNK], F32, name=f"state{c}") for c in range(CHUNKS)]
         x_rows = xT.rearrange("(p t) c -> p t c", t=PACK)
-        planes = [keep.tile([P, T], F32, name=f"plane{t}") for t in range(PACK)]
-        weight = keep.tile([P, J], F32, name="weight", align_bytes=64)
-        w_rows = keep.tile([P, 64], F32, name="w_rows", align_bytes=64)
-        w_turned = keep.tile([P, 64], F32, name="w_turned", align_bytes=64)
-        w_spread = keep.tile([P, J], F32, name="w_spread", align_bytes=64)
-        nc.sync.dma_start(w_rows[:], wgt[0:P:16, :].rearrange("g (i c) -> g i c", c=64))
-        nc.sync.dma_start(planes[0][:], x_rows[:, 0, :])
-        for b in range(2):
-            nc.vector.transpose(w_turned[:, 32 * b : 32 * b + 32], w_rows[:, 32 * b : 32 * b + 32])
-        for half in range(2):
-            js = slice(half * J // 2, (half + 1) * J // 2)
-            nc.vector.tensor_copy(
-                w_spread[:, js].rearrange("p (i b h r) -> p i b h r", b=2, h=2, r=16),
-                w_turned[:].rearrange("p (b h i) -> p i b h", b=2, h=2)[:, 8 * half : 8 * half + 8].unsqueeze(4).to_broadcast([P, 8, 2, 2, 16]),
-            )
-        for half in range(2):
-            js = slice(half * J // 2, (half + 1) * J // 2)
-            nc.vector.transpose(weight[:, js], w_spread[:, js])
-        nc.sync.dma_start(wv_raw[:].bitcast(I32), wv_words[0].bitcast(I32))
-        nc.sync.dma_start(planes[1][:], x_rows[:, 1, :])
-        nc.sync.dma_start(wk_raw[:], wk_words[0].rearrange("p n i -> p (n i)").bitcast(I32))
+        st_rows = st.rearrange("(p t) j -> p t j", t=PACK)
+        out_rows = out_0.rearrange("(p t) j -> p t j", t=PACK)
+        out_words = out_1[0].rearrange("p j i -> p (j i)").bitcast(I32)
 
         def load_scales(q):
             for first, rows in ((0, wv_scales), (4, wk_scales)):
                 at = 32 * q + first
                 nc.sync.dma_start(ws_raw[at : at + 4, :].bitcast(I32), rows[0, 4 * q : 4 * q + 4, :].bitcast(I32))
 
+        nc.gpsimd.memset(ws_raw.bitcast(I32), 0)
+        nc.sync.dma_start(offsets[:], offs)
+        nc.sync.dma_start(w_rows[:], wgt[0:P:GROUP, :].rearrange("g (i c) -> g i c", i=GROUP))
+        nc.sync.dma_start(planes[0][:], x_rows[:, 0, :])
+        nc.sync.dma_start(wv_raw[:].bitcast(I32), wv_words[0].bitcast(I32))
+        nc.sync.dma_start(planes[1][:], x_rows[:, 1, :])
+        nc.sync.dma_start(wk_raw[:], wk_words[0].rearrange("p n i -> p (n i)").bitcast(I32))
         nc.sync.dma_start(planes[2][:], x_rows[:, 2, :])
         load_scales(0)
         nc.sync.dma_start(planes[3][:], x_rows[:, 3, :])
         for q in range(1, 4):
             load_scales(q)
-        st_rows = st.rearrange("(p t) j -> p t j", t=PACK)
-        state = [keep.tile([P, PACK, CHUNK], F32, name=f"state{c}") for c in range(CHUNKS)]
         for c in range(CHUNKS):
-            nc.sync.dma_start(state[c][:], st_rows[:, :, c * CHUNK : (c + 1) * CHUNK])
+            nc.sync.dma_start(state[c][:], st_rows[:, :, chunk_cols(c)])
+
+        w_turned = keep.tile([P, J // GROUP], F32, name="w_turned", align_bytes=64)
+        w_spread = keep.tile([P, J], F32, name="w_spread", align_bytes=64)
+        weight = keep.tile([P, J], F32, name="weight", align_bytes=64)
+        halves = [slice(0, J // 2), slice(J // 2, J)]
+        for b in range(2):
+            square = slice(SQUARE * b, SQUARE * (b + 1))
+            nc.vector.transpose(w_turned[:, square], w_rows[:, square])
+        by_run = w_turned[:].rearrange("p (b h i) -> p i b h", b=2, h=2)
+        for n, js in enumerate(halves):
+            nc.vector.tensor_copy(
+                w_spread[:, js].rearrange("p (i b h r) -> p i b h r", b=2, h=2, r=GROUP),
+                by_run[:, 8 * n : 8 * n + 8].unsqueeze(4).to_broadcast([P, 8, 2, 2, GROUP]),
+            )
+        for js in halves:
+            nc.vector.transpose(weight[:, js], w_spread[:, js])
 
         wk = keep.tile([P, PACK, P], I32, name="wk", align_bytes=64)
         wv = keep.tile([P, PACK, P], U16, name="wv", align_bytes=64)
         ws = keep.tile([P, PACK, P], U8, name="ws", align_bytes=64)
-
-        def deal(dealt, raw):
-            nc.vector.tensor_copy(dealt.rearrange("p t m -> p m t"), raw.rearrange("p (m t) -> p m t", t=PACK))
-
         low = keep.tile([P, 2, J], F32, name="low")
         shared = keep.tile([P, 2 * J + CHUNK], F32, name="shared", align_bytes=64)
         high = shared[:, : 2 * J].rearrange("p (t j) -> p t j", t=2)
         xg = [shared[:, 2 * J - CHUNK :].bitcast(BF16).rearrange("p (j t) -> p j t", t=PACK)]
         xg.extend(keep.tile([P, CHUNK, PACK], BF16, name=f"xg{c}", align_bytes=64)[:] for c in range(1, CHUNKS))
         x_codes = [keep.tile([P, CHUNK], I32, name=f"x_codes{c}", align_bytes=64) for c in range(CHUNKS)]
-        x_scales = [all_scales[:, c * CHUNK : (c + 1) * CHUNK] for c in range(CHUNKS)]
-        y = [keep.tile([P, PACK, CHUNK], F32, name=f"y{c}") for c in range(CHUNKS)]
-        y_codes = keep.tile([P, J], I32, name="y_codes", align_bytes=64)
-        y_scales = keep.tile([P, J], U8, name="y_scales", align_bytes=64)
 
-        def gather(out, t, j0, j1):
-            nc.vector.tensor_tensor(out, planes[t][:].indirect(offsets[:, j0 // 16 : j1 // 16]), weight[:, j0:j1], MULT)
+        def deal(dealt, raw):
+            nc.vector.tensor_copy(dealt.rearrange("p t m -> p m t"), raw.rearrange("p (m t) -> p m t", t=PACK))
 
-        def gather_high(t, c):
-            gather(high[:, t - 2, c * CHUNK : (c + 1) * CHUNK], t, c * CHUNK, (c + 1) * CHUNK)
+        def gather(pair, t, js):
+            picked = planes[t][:].indirect(offsets[:, js.start // GROUP : js.stop // GROUP])
+            nc.vector.tensor_tensor(pair[:, t % 2, js], picked, weight[:, js], MULT)
 
-        def weave_low(c):
-            nc.scalar.copy(xg[c][:, :, 0:2], low[:, :, c * CHUNK : (c + 1) * CHUNK].rearrange("p t j -> p j t"))
-
-        def weave_high(c):
-            nc.scalar.copy(xg[c][:, :, 2:4], high[:, :, c * CHUNK : (c + 1) * CHUNK].rearrange("p t j -> p j t"))
+        def weave_x(pair, first, c):
+            nc.scalar.copy(xg[c][:, :, first : first + 2], pair[:, :, chunk_cols(c)].rearrange("p t j -> p j t"))
 
         def quantize_x(c):
             nc.vector.quantize_mx(
-                out=x_codes[c][:].bitcast(FP8X4), scales=x_scales[c], in_=xg[c].rearrange("p j t -> p (j t)")
+                out=x_codes[c][:].bitcast(FP8X4), scales=x_scales[:, chunk_cols(c)],
+                in_=xg[c].rearrange("p j t -> p (j t)"),
             )
 
-        ke, ve, gate = {}, {}, {}
-        first = keep.tile([P, 2 * CHUNK, PACK], BF16, name="woven_first", align_bytes=64)
-        woven = {0: first[:, :CHUNK, :], 1: first[:, CHUNK:, :]}
-        woven[2] = keep.tile([P, CHUNK, PACK], BF16, name="woven_third", align_bytes=64)
-        woven[3] = keep.tile([P, CHUNK, PACK], BF16, name="woven_last", align_bytes=64)
-
-        def place(u):
-            c, j0 = divmod(u * UNIT, CHUNK)
-            return c, slice(j0, j0 + UNIT)
-
-        def multiply(u):
-            c, cols = place(u)
-            ke[u] = key_banks.tile([P, PACK, UNIT], F32, name="ke")
-            ve[u] = value_banks.tile([P, PACK, UNIT], F32, name="ve")
-            for t in range(PACK):
-                nc.tensor.matmul_mx(
-                    out=ke[u][:, t, :], lhsT=wk[:, t, :].bitcast(FP8X4), lhsT_scale=ws[4:P, t, :],
-                    rhs=x_codes[c][:, cols].bitcast(FP8X4), rhs_scale=x_scales[c][:, cols], start=True, stop=True,
-                )
-            for t in range(PACK):
-                nc.tensor.matmul_mx(
-                    out=ve[u][:, t, :], lhsT=wv[:, t, :].bitcast(FP4X4),
-                    lhsT_scale=ws[:, t, :],
-                    rhs=x_codes[c][:, cols].bitcast(FP8X4), rhs_scale=x_scales[c][:, cols], start=True, stop=True,
-                )
-
-        def open_gate(u):
-            c, cols = place(u)
-            logit = ring.tile([P, PACK, UNIT], F32, name="logit")
-            gate[u] = ring.tile([P, PACK, UNIT], F32, name="gate")
-            if u in POOL_PRODUCT:
-                held = ring.tile([P, PACK, UNIT], F32, name="held")
-                nc.scalar.copy(held[:], ve[u][:])
-                ve[u] = held
-            nc.vector.tensor_tensor(logit[:], ke[u][:], state[c][:, :, cols], MULT)
-            nc.scalar.activation(gate[u][:], logit[:], TANH)
-
-        ones = keep.tile([P, PACK, UNIT], F32, name="ones")
-        nc.gpsimd.memset(ones[:], 1.0)
-
-        def weave_y(engine, c, cols):
-            out = woven[c][:, cols, :].rearrange("p (a i) t -> p a t i", i=4)
-            src = y[c][:, :, cols].rearrange("p t (a i) -> p a t i", i=4)
-            if engine == "pool":
-                nc.gpsimd.tensor_tensor(out, src, ones[:].rearrange("p t (a i) -> p a t i", i=4), MULT)
-            elif engine == "act":
-                nc.scalar.copy(out, src)
-            else:
-                nc.vector.tensor_copy(out, src)
-
-        def quantize_cols(c, cols):
-            js = slice(c * CHUNK + cols.start, c * CHUNK + cols.stop)
-            nc.vector.quantize_mx(
-                out=y_codes[:, js].bitcast(FP8X4), scales=y_scales[:, js],
-                in_=woven[c][:, cols, :].rearrange("p j t -> p (j t)"),
-            )
-
-        def let_through(u):
-            c, cols = place(u)
-            if u in POOL_PRODUCT:
-                nc.gpsimd.tensor_tensor(y[c][:, :, cols], ve[u][:], gate[u][:], MULT)
-            else:
-                nc.vector.tensor_tensor(y[c][:, :, cols], ve[u][:], gate[u][:], MULT)
-            weave_y("pool" if u in POOL_WEAVE else "act", c, cols)
-            if c >= CHUNKS - 2:
-                nc.sync.dma_start(out_rows[:, :, u * UNIT : (u + 1) * UNIT], y[c][:, :, cols])
-            elif cols.stop == CHUNK:
-                nc.sync.dma_start(out_rows[:, :, c * CHUNK : (c + 1) * CHUNK], y[c][:])
-
-        def quantize_y(c):
-            quantize_cols(c, slice(0, CHUNK))
-            js = slice(c * CHUNK, (c + 1) * CHUNK)
-            nc.sync.dma_start(out_words[:, js], y_codes[:, js])
-
-        def quantize_first():
-            js = slice(0, 2 * CHUNK)
-            nc.vector.quantize_mx(
-                out=y_codes[:, js].bitcast(FP8X4), scales=y_scales[:, js], in_=first[:].rearrange("p j t -> p (j t)")
-            )
-            nc.sync.dma_start(out_words[:, js], y_codes[:, js])
-
-        def finish():
-            u = UNITS - 1
-            c, cols = place(u)
-            halves = [slice(0, UNIT // 2), slice(UNIT // 2, UNIT)]
-            placed = [slice(cols.start + h.start, cols.start + h.stop) for h in halves]
-            for h, at in zip(halves, placed):
-                nc.vector.tensor_tensor(y[c][:, :, at], ve[u][:, :, h], gate[u][:, :, h], MULT)
-            weave_y("act", c, placed[0])
-            nc.sync.dma_start(out_rows[:, :, u * UNIT :], y[c][:, :, cols])
-            quantize_cols(c, slice(0, UNIT))
-            weave_y("vector", c, placed[1])
-            for at in placed:
-                quantize_cols(c, at)
-            nc.sync.dma_start(out_words[:, c * CHUNK :], y_codes[:, c * CHUNK :])
-
-        out_rows = out_0.rearrange("(p t) j -> p t j", t=PACK)
-        out_words = out_1[0].rearrange("p j i -> p (j i)").bitcast(I32)
-
-        gather(low[:, 0, : J // 2], 0, 0, J // 2)
-        gather(low[:, 0, J // 2 :], 0, J // 2, J)
+        for js in halves:
+            gather(low, 0, js)
         deal(wv[:], wv_raw[:].bitcast(U16))
-        gather(low[:, 1, : J // 2], 1, 0, J // 2)
-        gather(low[:, 1, J // 2 :], 1, J // 2, J)
+        for js in halves:
+            gather(low, 1, js)
         deal(wk[:], wk_raw[:])
         for c in range(CHUNKS):
-            weave_low(c)
-        gather(high[:, 0, :], 2, 0, J)
+            weave_x(low, 0, c)
+        gather(high, 2, slice(0, J))
         for c in range(CHUNKS - 1):
-            gather_high(3, c)
-            weave_high(c)
+            gather(high, 3, chunk_cols(c))
+            weave_x(high, 2, c)
         deal(ws[:], ws_raw)
         quantize_x(0)
-        gather_high(3, CHUNKS - 1)
-        weave_high(CHUNKS - 1)
+        gather(high, 3, chunk_cols(CHUNKS - 1))
+        weave_x(high, 2, CHUNKS - 1)
         quantize_x(1)
         quantize_x(2)
-        for s in range(UNITS):
-            multiply(s)
-            open_gate(s)
-            if s == 0:
+
+        y = [keep.tile([P, PACK, CHUNK], F32, name=f"y{c}") for c in range(CHUNKS)]
+        woven = keep.tile([P, J, PACK], BF16, name="woven", align_bytes=64)
+        y_codes = keep.tile([P, J], I32, name="y_codes", align_bytes=64)
+        y_scales = keep.tile([P, J], U8, name="y_scales", align_bytes=64)
+        held = [keep.tile([P, PAIR, CHUNK], F32, name="held_first")[:]]
+        held.append(
+            woven[:, :CHUNK, :].rearrange("p j t -> p (j t)").bitcast(F32).rearrange("p (t j) -> p t j", t=PAIR)
+        )
+        ke, ve, gate = {}, {}, {}
+
+        def place(u):
+            c, h = divmod(u, PACK // PAIR)
+            return c, slice(PAIR * h, PAIR * (h + 1))
+
+        def multiply(u):
+            c, ts = place(u)
+            ke[u] = key_banks.tile([P, PAIR, CHUNK], F32, name="ke")
+            ve[u] = value_banks.tile([P, PAIR, CHUNK], F32, name="ve")
+            for out, words, packed, row in ((ke[u], wk, FP8X4, 4), (ve[u], wv, FP4X4, 0)):
+                for t in range(ts.start, ts.stop):
+                    nc.tensor.matmul_mx(
+                        out=out[:, t - ts.start, :], lhsT=words[:, t, :].bitcast(packed), lhsT_scale=ws[row:P, t, :],
+                        rhs=x_codes[c][:].bitcast(FP8X4), rhs_scale=x_scales[:, chunk_cols(c)], start=True, stop=True,
+                    )
+
+        def open_gate(u):
+            c, ts = place(u)
+            logit = ring.tile([P, PAIR, CHUNK], F32, name="logit")
+            gate[u] = ring.tile([P, PAIR, CHUNK], F32, name="gate")
+            if u < GPSIMD_UNITS:
+                nc.scalar.copy(held[u], ve[u][:])
+            nc.vector.tensor_tensor(logit[:], ke[u][:], state[c][:, ts, :], MULT)
+            nc.scalar.activation(gate[u][:], logit[:], TANH)
+
+        def weave_y(c, n):
+            cols = slice(n * HALF, (n + 1) * HALF)
+            out = woven[:, c * CHUNK + cols.start : c * CHUNK + cols.stop, :]
+            if c < GPSIMD_CHUNKS:
+                nc.gpsimd.tensor_scalar(out, y[c][:, :, cols].rearrange("p t j -> p j t"), 1.0, -0.0, MULT, ADD)
+            else:
+                nc.scalar.copy(
+                    out.rearrange("p (a i) t -> p a t i", i=4), y[c][:, :, cols].rearrange("p t (a i) -> p a t i", i=4)
+                )
+
+        def let_through(u):
+            c, ts = place(u)
+            if u < GPSIMD_UNITS:
+                nc.gpsimd.tensor_tensor(y[c][:, ts, :], held[u], gate[u][:], MULT)
+            else:
+                nc.vector.tensor_tensor(y[c][:, ts, :], ve[u][:], gate[u][:], MULT)
+            nc.sync.dma_start(out_rows[:, ts, chunk_cols(c)], y[c][:, ts, :])
+            if ts.stop == PACK:
+                for n in range(2):
+                    weave_y(c, n)
+
+        def quantize_y(js):
+            nc.vector.quantize_mx(
+                out=y_codes[:, js].bitcast(FP8X4), scales=y_scales[:, js],
+                in_=woven[:, js, :].rearrange("p j t -> p (j t)"),
+            )
+
+        def store_words(js):
+            nc.sync.dma_start(out_words[:, js], y_codes[:, js])
+
+        for u in range(UNITS):
+            multiply(u)
+            open_gate(u)
+            if u == 0:
                 quantize_x(CHUNKS - 1)
-            if s >= 2:
-                let_through(s - 2)
-        quantize_first()
-        let_through(UNITS - 2)
-        quantize_y(CHUNKS - 2)
-        finish()
+            if u >= LAG:
+                let_through(u - LAG)
+        for u in range(UNITS - LAG, UNITS - 1):
+            let_through(u)
+        c, ts = place(UNITS - 1)
+        for n in range(2):
+            cols = slice(n * HALF, (n + 1) * HALF)
+            nc.vector.tensor_tensor(y[c][:, ts, cols], ve[UNITS - 1][:, :, cols], gate[UNITS - 1][:, :, cols], MULT)
+            weave_y(c, n)
+        nc.sync.dma_start(out_rows[:, ts, chunk_cols(c)], y[c][:, ts, :])
+        for js in (halves[0], chunk_cols(CHUNKS - 2)):
+            quantize_y(js)
+            store_words(js)
+        quantize_y(slice(J - CHUNK, J - HALF))
+        quantize_y(slice(J - HALF, J))
+        store_words(chunk_cols(CHUNKS - 1))
         for q in range(4):
             queue = nc.scalar if q % 2 else nc.sync
             queue.dma_start(

@@ -26,8 +26,10 @@ PAIR = 2
 UNITS = CHUNKS * PACK // PAIR
 HALF = CHUNK // 2
 LAG = 2
-GPSIMD_UNITS = 2
-GPSIMD_CHUNKS = 2
+EARLY_SCALES = 5
+GPSIMD_PRODUCTS = (0, 2)
+GPSIMD_WEAVES = ((1, 0), (1, 1), (2, 0))
+BANK = 512
 
 
 def tile_list_tanhP_kernel(
@@ -43,6 +45,12 @@ def tile_list_tanhP_kernel(
         def chunk_cols(c):
             return slice(c * CHUNK, (c + 1) * CHUNK)
 
+        def place(u):
+            c, h = divmod(u, 2)
+            if c < CHUNKS // 2:
+                return c, slice(PAIR * h, PAIR * (h + 1)), slice(0, CHUNK)
+            return c, slice(0, PACK), slice(HALF * h, HALF * (h + 1))
+
         offsets = keep.tile([P, J // GROUP], U16, name="offsets")
         w_rows = keep.tile([P, J // GROUP], F32, name="w_rows", align_bytes=64)
         planes = [keep.tile([P, T], F32, name=f"plane{t}") for t in range(PACK)]
@@ -50,31 +58,39 @@ def tile_list_tanhP_kernel(
         wv_raw = keep.tile([P, 2 * N], U8, name="wv_raw")
         x_scales = keep.tile([P, J], U8, name="x_scales", align_bytes=64)
         ws_raw = x_scales[:, HALF : HALF + N]
-        state = [keep.tile([P, PACK, CHUNK], F32, name=f"state{c}") for c in range(CHUNKS)]
         x_rows = xT.rearrange("(p t) c -> p t c", t=PACK)
         st_rows = st.rearrange("(p t) j -> p t j", t=PACK)
         out_rows = out_0.rearrange("(p t) j -> p t j", t=PACK)
         out_words = out_1[0].rearrange("p j i -> p (j i)").bitcast(I32)
 
-        def load_scales(q):
-            for first, rows in ((0, wv_scales), (4, wk_scales)):
-                at = 32 * q + first
-                nc.sync.dma_start(ws_raw[at : at + 4, :].bitcast(I32), rows[0, 4 * q : 4 * q + 4, :].bitcast(I32))
+        def load_scales(n):
+            q, first = n // 2, 4 * (n % 2)
+            rows = wk_scales if first else wv_scales
+            at = 32 * q + first
+            nc.sync.dma_start(ws_raw[at : at + 4, :].bitcast(I32), rows[0, 4 * q : 4 * q + 4, :].bitcast(I32))
 
         nc.gpsimd.memset(ws_raw.bitcast(I32), 0)
-        nc.sync.dma_start(offsets[:], offs)
         nc.sync.dma_start(w_rows[:], wgt[0:P:GROUP, :].rearrange("g (i c) -> g i c", i=GROUP))
+        nc.sync.dma_start(offsets[:], offs)
         nc.sync.dma_start(planes[0][:], x_rows[:, 0, :])
-        nc.sync.dma_start(wv_raw[:].bitcast(I32), wv_words[0].bitcast(I32))
         nc.sync.dma_start(planes[1][:], x_rows[:, 1, :])
         nc.sync.dma_start(wk_raw[:], wk_words[0].rearrange("p n i -> p (n i)").bitcast(I32))
         nc.sync.dma_start(planes[2][:], x_rows[:, 2, :])
-        load_scales(0)
+        for n in range(EARLY_SCALES):
+            load_scales(n)
         nc.sync.dma_start(planes[3][:], x_rows[:, 3, :])
-        for q in range(1, 4):
-            load_scales(q)
-        for c in range(CHUNKS):
-            nc.sync.dma_start(state[c][:], st_rows[:, :, chunk_cols(c)])
+        for n in range(EARLY_SCALES, 8):
+            load_scales(n)
+        nc.sync.dma_start(wv_raw[:].bitcast(I32), wv_words[0].bitcast(I32))
+        state = {}
+        for u in range(2):
+            state[u] = keep.tile([P, PAIR, CHUNK], F32, name=f"state_unit{u}", align_bytes=64)[:]
+            nc.sync.dma_start(state[u], st_rows[:, PAIR * u : PAIR * (u + 1), chunk_cols(0)])
+        for c in range(1, CHUNKS):
+            both = keep.tile([P, PACK, CHUNK], F32, name=f"state_chunk{c}")
+            nc.sync.dma_start(both[:], st_rows[:, :, chunk_cols(c)])
+            for u in range(2 * c, 2 * c + 2):
+                state[u] = both[:, place(u)[1], place(u)[2]]
 
         w_turned = keep.tile([P, J // GROUP], F32, name="w_turned", align_bytes=64)
         w_spread = keep.tile([P, J], F32, name="w_spread", align_bytes=64)
@@ -96,11 +112,11 @@ def tile_list_tanhP_kernel(
         wv = keep.tile([P, PACK, P], U16, name="wv", align_bytes=64)
         ws = keep.tile([P, PACK, P], U8, name="ws", align_bytes=64)
         low = keep.tile([P, 2, J], F32, name="low")
-        shared = keep.tile([P, 2 * J + CHUNK], F32, name="shared", align_bytes=64)
-        high = shared[:, : 2 * J].rearrange("p (t j) -> p t j", t=2)
-        xg = [shared[:, 2 * J - CHUNK :].bitcast(BF16).rearrange("p (j t) -> p j t", t=PACK)]
+        shared = keep.tile([P, 2 * J], F32, name="shared", align_bytes=64)
+        high = shared[:].rearrange("p (t j) -> p t j", t=2)
+        xg = [shared[:, 2 * J - 2 * CHUNK :].bitcast(BF16).rearrange("p (j t) -> p j t", t=PACK)]
         xg.extend(keep.tile([P, CHUNK, PACK], BF16, name=f"xg{c}", align_bytes=64)[:] for c in range(1, CHUNKS))
-        x_codes = [keep.tile([P, CHUNK], I32, name=f"x_codes{c}", align_bytes=64) for c in range(CHUNKS)]
+        x_codes = [keep.tile([P, CHUNK], I32, name=f"x_codes{c}", align_bytes=64) for c in range(2)]
 
         def deal(dealt, raw):
             nc.vector.tensor_copy(dealt.rearrange("p t m -> p m t"), raw.rearrange("p (m t) -> p m t", t=PACK))
@@ -120,77 +136,83 @@ def tile_list_tanhP_kernel(
 
         for js in halves:
             gather(low, 0, js)
-        deal(wv[:], wv_raw[:].bitcast(U16))
         for js in halves:
             gather(low, 1, js)
         deal(wk[:], wk_raw[:])
         for c in range(CHUNKS):
             weave_x(low, 0, c)
         gather(high, 2, slice(0, J))
-        for c in range(CHUNKS - 1):
+        for js in (slice(0, HALF), slice(HALF, CHUNK)):
+            gather(high, 3, js)
+            nc.scalar.copy(xg[0][:, js, 2:4], high[:, :, js].rearrange("p t j -> p j t"))
+        deal(ws[:], ws_raw)
+        gather(high, 3, chunk_cols(1))
+        weave_x(high, 2, 1)
+        quantize_x(0)
+        deal(wv[:], wv_raw[:].bitcast(U16))
+        for c in range(2, CHUNKS):
             gather(high, 3, chunk_cols(c))
             weave_x(high, 2, c)
-        deal(ws[:], ws_raw)
-        quantize_x(0)
-        gather(high, 3, chunk_cols(CHUNKS - 1))
-        weave_x(high, 2, CHUNKS - 1)
         quantize_x(1)
-        quantize_x(2)
 
-        y = [keep.tile([P, PACK, CHUNK], F32, name=f"y{c}") for c in range(CHUNKS)]
-        woven = keep.tile([P, J, PACK], BF16, name="woven", align_bytes=64)
+        y = {c: keep.tile([P, PACK, CHUNK], F32, name=f"y{c}") for c in range(1, CHUNKS)}
+        padded = keep.tile([P, HALF + J, PACK], BF16, name="woven", align_bytes=64)
+        woven = padded[:, HALF:, :]
         y_codes = keep.tile([P, J], I32, name="y_codes", align_bytes=64)
         y_scales = keep.tile([P, J], U8, name="y_scales", align_bytes=64)
-        held = [keep.tile([P, PAIR, CHUNK], F32, name="held_first")[:]]
-        held.append(
-            woven[:, :CHUNK, :].rearrange("p j t -> p (j t)").bitcast(F32).rearrange("p (t j) -> p t j", t=PAIR)
-        )
+        held = {u: keep.tile([P, PAIR, CHUNK], F32, name=f"held{u}")[:] for u in GPSIMD_PRODUCTS}
         ke, ve, gate = {}, {}, {}
 
-        def place(u):
-            c, h = divmod(u, PACK // PAIR)
-            return c, slice(PAIR * h, PAIR * (h + 1))
+        def shaped(tile, u):
+            ts = place(u)[1]
+            return tile[:].rearrange("p (t j) -> p t j", t=ts.stop - ts.start)
 
-        def multiply(u):
-            c, ts = place(u)
-            ke[u] = key_banks.tile([P, PAIR, CHUNK], F32, name="ke")
-            ve[u] = value_banks.tile([P, PAIR, CHUNK], F32, name="ve")
-            for out, words, packed, row in ((ke[u], wk, FP8X4, 4), (ve[u], wv, FP4X4, 0)):
-                for t in range(ts.start, ts.stop):
-                    nc.tensor.matmul_mx(
-                        out=out[:, t - ts.start, :], lhsT=words[:, t, :].bitcast(packed), lhsT_scale=ws[row:P, t, :],
-                        rhs=x_codes[c][:].bitcast(FP8X4), rhs_scale=x_scales[:, chunk_cols(c)], start=True, stop=True,
-                    )
+        def multiply(u, banks, name, words, packed, row):
+            c, ts, cols = place(u)
+            js = slice(c * CHUNK + cols.start, c * CHUNK + cols.stop)
+            out = shaped(banks.tile([P, BANK], F32, name=name), u)
+            for t in range(ts.start, ts.stop):
+                nc.tensor.matmul_mx(
+                    out=out[:, t - ts.start, :], lhsT=words[:, t, :].bitcast(packed), lhsT_scale=ws[row:P, t, :],
+                    rhs=x_codes[c][:, cols].bitcast(FP8X4), rhs_scale=x_scales[:, js], start=True, stop=True,
+                )
+            return out
 
         def open_gate(u):
-            c, ts = place(u)
-            logit = ring.tile([P, PAIR, CHUNK], F32, name="logit")
-            gate[u] = ring.tile([P, PAIR, CHUNK], F32, name="gate")
-            if u < GPSIMD_UNITS:
-                nc.scalar.copy(held[u], ve[u][:])
-            nc.vector.tensor_tensor(logit[:], ke[u][:], state[c][:, ts, :], MULT)
-            nc.scalar.activation(gate[u][:], logit[:], TANH)
+            if u == UNITS - 1:
+                logit = padded[:, :CHUNK, :].rearrange("p j t -> p (j t)").bitcast(F32).rearrange("p (t j) -> p t j", t=PACK)
+            else:
+                logit = shaped(ring.tile([P, BANK], F32, name="logit"), u)
+            gate[u] = shaped(ring.tile([P, BANK], F32, name="gate"), u)
+            if u in GPSIMD_PRODUCTS:
+                nc.scalar.copy(held[u], ve[u])
+            nc.vector.tensor_tensor(logit, ke[u], state[u], MULT)
+            nc.scalar.activation(gate[u], logit, TANH)
 
         def weave_y(c, n):
             cols = slice(n * HALF, (n + 1) * HALF)
             out = woven[:, c * CHUNK + cols.start : c * CHUNK + cols.stop, :]
-            if c < GPSIMD_CHUNKS:
+            if (c, n) in GPSIMD_WEAVES:
                 nc.gpsimd.tensor_scalar(out, y[c][:, :, cols].rearrange("p t j -> p j t"), 1.0, -0.0, MULT, ADD)
             else:
-                nc.scalar.copy(
+                copy = nc.vector.tensor_copy if (c, n) == (CHUNKS - 1, 1) else nc.scalar.copy
+                copy(
                     out.rearrange("p (a i) t -> p a t i", i=4), y[c][:, :, cols].rearrange("p t (a i) -> p a t i", i=4)
                 )
 
         def let_through(u):
-            c, ts = place(u)
-            if u < GPSIMD_UNITS:
-                nc.gpsimd.tensor_tensor(y[c][:, ts, :], held[u], gate[u][:], MULT)
+            c, ts, cols = place(u)
+            if u in GPSIMD_PRODUCTS:
+                nc.gpsimd.tensor_tensor(y[c][:, ts, cols], held[u], gate[u], MULT)
             else:
-                nc.vector.tensor_tensor(y[c][:, ts, :], ve[u][:], gate[u][:], MULT)
-            nc.sync.dma_start(out_rows[:, ts, chunk_cols(c)], y[c][:, ts, :])
+                nc.vector.tensor_tensor(y[c][:, ts, cols], ve[u], gate[u], MULT)
+            nc.sync.dma_start(
+                out_rows[:, ts, c * CHUNK + cols.start : c * CHUNK + cols.stop], y[c][:, ts, cols]
+            )
             if ts.stop == PACK:
-                for n in range(2):
-                    weave_y(c, n)
+                for n in range(cols.start // HALF, cols.stop // HALF):
+                    if (c, n) not in ((0, 0), (CHUNKS - 1, 1)):
+                        weave_y(c, n)
 
         def quantize_y(js):
             nc.vector.quantize_mx(
@@ -201,26 +223,31 @@ def tile_list_tanhP_kernel(
         def store_words(js):
             nc.sync.dma_start(out_words[:, js], y_codes[:, js])
 
+        ke[0] = multiply(0, key_banks, "ke", wk, FP8X4, 4)
         for u in range(UNITS):
-            multiply(u)
+            if u + 1 < UNITS:
+                ke[u + 1] = multiply(u + 1, key_banks, "ke", wk, FP8X4, 4)
+            ve[u] = multiply(u, value_banks, "ve", wv, FP4X4, 0)
             open_gate(u)
-            if u == 0:
-                quantize_x(CHUNKS - 1)
+            if u == 1:
+                for c in range(2, CHUNKS):
+                    x_codes.append(
+                        keep.tile([P, CHUNK], I32, name=f"x_codes{c}", tag=f"state_unit{c - 2}", align_bytes=64)
+                    )
+                    quantize_x(c)
+                y[0] = keep.tile([P, PACK, CHUNK], F32, name="y0", tag=f"xg{CHUNKS - 1}", align_bytes=64)
+            if u == UNITS - 1:
+                weave_y(0, 0)
             if u >= LAG:
                 let_through(u - LAG)
-        for u in range(UNITS - LAG, UNITS - 1):
+        for u in range(UNITS - LAG, UNITS):
             let_through(u)
-        c, ts = place(UNITS - 1)
-        for n in range(2):
-            cols = slice(n * HALF, (n + 1) * HALF)
-            nc.vector.tensor_tensor(y[c][:, ts, cols], ve[UNITS - 1][:, :, cols], gate[UNITS - 1][:, :, cols], MULT)
-            weave_y(c, n)
-        nc.sync.dma_start(out_rows[:, ts, chunk_cols(c)], y[c][:, ts, :])
-        for js in (halves[0], chunk_cols(CHUNKS - 2)):
-            quantize_y(js)
-            store_words(js)
-        quantize_y(slice(J - CHUNK, J - HALF))
-        quantize_y(slice(J - HALF, J))
+        quantize_y(halves[0])
+        store_words(halves[0])
+        weave_y(CHUNKS - 1, 1)
+        quantize_y(chunk_cols(CHUNKS - 2))
+        store_words(chunk_cols(CHUNKS - 2))
+        quantize_y(chunk_cols(CHUNKS - 1))
         store_words(chunk_cols(CHUNKS - 1))
         for q in range(4):
             queue = nc.scalar if q % 2 else nc.sync

@@ -38,7 +38,7 @@ def tile_list_tanhP_kernel(
     nc = tc.nc
     with ExitStack() as ctx:
         keep = ctx.enter_context(tc.tile_pool(name="keep", bufs=1))
-        ring = ctx.enter_context(tc.tile_pool(name="ring", bufs=5))
+        ring = ctx.enter_context(tc.tile_pool(name="ring", bufs=UNITS))
         key_banks = ctx.enter_context(tc.psum_pool(name="key_banks", bufs=3))
         value_banks = ctx.enter_context(tc.psum_pool(name="value_banks", bufs=5))
 
@@ -145,7 +145,8 @@ def tile_list_tanhP_kernel(
         for js in (slice(0, HALF), slice(HALF, CHUNK)):
             gather(high, 3, js)
             nc.scalar.copy(xg[0][:, js, 2:4], high[:, :, js].rearrange("p t j -> p j t"))
-        deal(ws[:], ws_raw)
+        for n in range(2):
+            deal(ws[:, :, n * P // 2 : (n + 1) * P // 2], ws_raw[:, n * N // 2 : (n + 1) * N // 2])
         gather(high, 3, chunk_cols(1))
         weave_x(high, 2, 1)
         quantize_x(0)
@@ -250,7 +251,7 @@ def tile_list_tanhP_kernel(
         quantize_y(chunk_cols(CHUNKS - 1))
         store_words(chunk_cols(CHUNKS - 1))
         for q in range(4):
-            queue = nc.scalar if q % 2 else nc.sync
+            queue = nc.scalar if q // 2 else nc.sync
             queue.dma_start(
                 out_2[0, 4 * q : 4 * q + 4, :].bitcast(I32), y_scales[32 * q : 32 * q + 4, :].bitcast(I32)
             )

@@ -25,10 +25,10 @@ CHUNKS = J // CHUNK
 PAIR = 2
 UNITS = CHUNKS * PACK // PAIR
 HALF = CHUNK // 2
-LAG = 2
+LAG = 3
 EARLY_SCALES = 5
-GPSIMD_PRODUCTS = (0, 2)
-GPSIMD_WEAVES = ((1, 0), (1, 1), (2, 0))
+GPSIMD_PRODUCTS = (0, 1)
+GPSIMD_WEAVES = ((0, 0), (0, 1), (1, 0))
 BANK = 512
 
 
@@ -157,8 +157,7 @@ def tile_list_tanhP_kernel(
         quantize_x(1)
 
         y = {c: keep.tile([P, PACK, CHUNK], F32, name=f"y{c}") for c in range(1, CHUNKS)}
-        padded = keep.tile([P, HALF + J, PACK], BF16, name="woven", align_bytes=64)
-        woven = padded[:, HALF:, :]
+        woven = keep.tile([P, J, PACK], BF16, name="woven", align_bytes=64)
         y_codes = keep.tile([P, J], I32, name="y_codes", align_bytes=64)
         y_scales = keep.tile([P, J], U8, name="y_scales", align_bytes=64)
         held = {u: keep.tile([P, PAIR, CHUNK], F32, name=f"held{u}")[:] for u in GPSIMD_PRODUCTS}
@@ -180,10 +179,7 @@ def tile_list_tanhP_kernel(
             return out
 
         def open_gate(u):
-            if u == UNITS - 1:
-                logit = padded[:, :CHUNK, :].rearrange("p j t -> p (j t)").bitcast(F32).rearrange("p (t j) -> p t j", t=PACK)
-            else:
-                logit = shaped(ring.tile([P, BANK], F32, name="logit"), u)
+            logit = shaped(ring.tile([P, BANK], F32, name="logit"), u)
             gate[u] = shaped(ring.tile([P, BANK], F32, name="gate"), u)
             if u in GPSIMD_PRODUCTS:
                 nc.scalar.copy(held[u], ve[u])
@@ -212,7 +208,7 @@ def tile_list_tanhP_kernel(
             )
             if ts.stop == PACK:
                 for n in range(cols.start // HALF, cols.stop // HALF):
-                    if (c, n) not in ((0, 0), (CHUNKS - 1, 1)):
+                    if (c, n) != (CHUNKS - 1, 1):
                         weave_y(c, n)
 
         def quantize_y(js):
@@ -237,8 +233,6 @@ def tile_list_tanhP_kernel(
                     )
                     quantize_x(c)
                 y[0] = keep.tile([P, PACK, CHUNK], F32, name="y0", tag=f"xg{CHUNKS - 1}", align_bytes=64)
-            if u == UNITS - 1:
-                weave_y(0, 0)
             if u >= LAG:
                 let_through(u - LAG)
         for u in range(UNITS - LAG, UNITS):

@@ -47,9 +47,7 @@ def tile_list_tanhP_kernel(
 
         def place(u):
             c, h = divmod(u, 2)
-            if c < CHUNKS // 2:
-                return c, slice(PAIR * h, PAIR * (h + 1)), slice(0, CHUNK)
-            return c, slice(0, PACK), slice(HALF * h, HALF * (h + 1))
+            return c, slice(PAIR * h, PAIR * (h + 1)), slice(0, CHUNK)
 
         offsets = keep.tile([P, J // GROUP], U16, name="offsets")
         w_rows = keep.tile([P, J // GROUP], F32, name="w_rows", align_bytes=64)

@@ -223,6 +223,8 @@ def tile_list_tanhP_kernel(
             if u + 1 < UNITS:
                 ke[u + 1] = multiply(u + 1, key_banks, "ke", wk, FP8X4, 4)
             ve[u] = multiply(u, value_banks, "ve", wv, FP4X4, 0)
+            if u >= UNITS - 2:
+                let_through(u - LAG)
             open_gate(u)
             if u == 1:
                 for c in range(2, CHUNKS):
@@ -231,7 +233,7 @@ def tile_list_tanhP_kernel(
                     )
                     quantize_x(c)
                 y[0] = keep.tile([P, PACK, CHUNK], F32, name="y0", tag=f"xg{CHUNKS - 1}", align_bytes=64)
-            if u >= LAG:
+            if LAG <= u < UNITS - 2:
                 let_through(u - LAG)
         for u in range(UNITS - LAG, UNITS):
             let_through(u)

@@ -98,12 +98,15 @@ def tile_list_tanhP_kernel(
             square = slice(SQUARE * b, SQUARE * (b + 1))
             nc.vector.transpose(w_turned[:, square], w_rows[:, square])
         by_run = w_turned[:].rearrange("p (b h i) -> p i b h", b=2, h=2)
-        for n, js in enumerate(halves):
-            nc.vector.tensor_copy(
+        parts = [chunk_cols(0), chunk_cols(1), halves[1]]
+        for js in parts:
+            runs = slice(js.start // (2 * SQUARE), js.stop // (2 * SQUARE))
+            copy = nc.scalar.copy if js == halves[1] else nc.vector.tensor_copy
+            copy(
                 w_spread[:, js].rearrange("p (i b h r) -> p i b h r", b=2, h=2, r=GROUP),
-                by_run[:, 8 * n : 8 * n + 8].unsqueeze(4).to_broadcast([P, 8, 2, 2, GROUP]),
+                by_run[:, runs].unsqueeze(4).to_broadcast([P, runs.stop - runs.start, 2, 2, GROUP]),
             )
-        for js in halves:
+        for js in parts:
             nc.vector.transpose(weight[:, js], w_spread[:, js])
 
         wk = keep.tile([P, PACK, P], I32, name="wk", align_bytes=64)

@@ -8,6 +8,7 @@ FLOPS = 2 * 2 * K * N * J
 F32 = mybir.dt.float32
 BF16 = mybir.dt.bfloat16
 I32 = mybir.dt.int32
+U32 = mybir.dt.uint32
 U16 = mybir.dt.uint16
 U8 = mybir.dt.uint8
 FP8X4 = mybir.dt.float8_e4m3fn_x4
@@ -52,7 +53,7 @@ def tile_list_tanhP_kernel(
         offsets = keep.tile([P, J // GROUP], U16, name="offsets")
         w_rows = keep.tile([P, J // GROUP], F32, name="w_rows", align_bytes=64)
         planes = [keep.tile([P, T], F32, name=f"plane{t}") for t in range(PACK)]
-        wk_raw = keep.tile([P, N], I32, name="wk_raw")
+        wk_raw = keep.tile([P, N], U32, name="wk_raw")
         wv_raw = keep.tile([P, 2 * N], U8, name="wv_raw")
         x_scales = keep.tile([P, J], U8, name="x_scales", align_bytes=64)
         ws_raw = x_scales[:, HALF : HALF + N]
@@ -68,11 +69,12 @@ def tile_list_tanhP_kernel(
             nc.sync.dma_start(ws_raw[at : at + 4, :].bitcast(I32), rows[0, 4 * q : 4 * q + 4, :].bitcast(I32))
 
         nc.gpsimd.memset(ws_raw.bitcast(I32), 0)
-        nc.sync.dma_start(w_rows[:], wgt[0:P:GROUP, :].rearrange("g (i c) -> g i c", i=GROUP))
+        half_rows = wgt.rearrange("r (h c) -> (r h) c", h=2)[0 : 2 * P : GROUP + 1, :]
+        nc.sync.dma_start(w_rows[:], half_rows.rearrange("u (v c) -> u v c", v=GROUP // 2))
         nc.sync.dma_start(offsets[:], offs)
         nc.sync.dma_start(planes[0][:], x_rows[:, 0, :])
         nc.sync.dma_start(planes[1][:], x_rows[:, 1, :])
-        nc.sync.dma_start(wk_raw[:], wk_words[0].rearrange("p n i -> p (n i)").bitcast(I32))
+        nc.sync.dma_start(wk_raw[:].bitcast(I32), wk_words[0].rearrange("p n i -> p (n i)").bitcast(I32))
         nc.sync.dma_start(planes[2][:], x_rows[:, 2, :])
         for n in range(EARLY_SCALES):
             load_scales(n)
@@ -109,7 +111,7 @@ def tile_list_tanhP_kernel(
         for js in parts:
             nc.vector.transpose(weight[:, js], w_spread[:, js])
 
-        wk = keep.tile([P, PACK, P], I32, name="wk", align_bytes=64)
+        wk = keep.tile([P, PACK, P], U32, name="wk", align_bytes=64)
         wv = keep.tile([P, PACK, P], U16, name="wv", align_bytes=64)
         ws = keep.tile([P, PACK, P], U8, name="ws", align_bytes=64)
         low = keep.tile([P, 2, J], F32, name="low")
@@ -139,7 +141,7 @@ def tile_list_tanhP_kernel(
             gather(low, 0, js)
         for js in halves:
             gather(low, 1, js)
-        deal(wk[:], wk_raw[:])
+        nc.scalar.copy(wk[:].rearrange("p t m -> p m t"), wk_raw[:].rearrange("p (m t) -> p m t", t=PACK))
         for c in range(CHUNKS):
             weave_x(low, 0, c)
         gather(high, 2, slice(0, J))

from contextlib import ExitStack

import concourse.mybir as mybir

K, N, T, J = 512, 512, 2048, 1024
FLOPS = 2 * 2 * K * N * J

F32 = mybir.dt.float32
BF16 = mybir.dt.bfloat16
I32 = mybir.dt.int32
U32 = mybir.dt.uint32
U16 = mybir.dt.uint16
U8 = mybir.dt.uint8
FP8X4 = mybir.dt.float8_e4m3fn_x4
FP4X4 = mybir.dt.float4_e2m1fn_x4
MULT = mybir.AluOpType.mult
ADD = mybir.AluOpType.add
TANH = mybir.ActivationFunctionType.Tanh

P = 128
PACK = 4
GROUP = 16
SQUARE = 32
CHUNK = 256
CHUNKS = J // CHUNK
PAIR = 2
UNITS = CHUNKS * PACK // PAIR
HALF = CHUNK // 2
LAG = 3
EARLY_SCALES = 5
GPSIMD_PRODUCTS = (0, 1)
GPSIMD_WEAVES = ((0, 0), (0, 1), (1, 0))
BANK = 512


def tile_list_tanhP_kernel(
    tc, xT, wgt, wk_words, wk_scales, wv_words, wv_scales, st, offs, out_0, out_1, out_2
):
    nc = tc.nc
    with ExitStack() as ctx:
        keep = ctx.enter_context(tc.tile_pool(name="keep", bufs=1))
        ring = ctx.enter_context(tc.tile_pool(name="ring", bufs=UNITS))
        key_banks = ctx.enter_context(tc.psum_pool(name="key_banks", bufs=3))
        value_banks = ctx.enter_context(tc.psum_pool(name="value_banks", bufs=5))

        def chunk_cols(c):
            return slice(c * CHUNK, (c + 1) * CHUNK)

        def place(u):
            c, h = divmod(u, 2)
            return c, slice(PAIR * h, PAIR * (h + 1)), slice(0, CHUNK)

        offsets = keep.tile([P, J // GROUP], U16, name="offsets")
        w_rows = keep.tile([P, J // GROUP], F32, name="w_rows", align_bytes=64)
        planes = [keep.tile([P, T], F32, name=f"plane{t}") for t in range(PACK)]
        wk_raw = keep.tile([P, N], U32, name="wk_raw")
        wv_raw = keep.tile([P, 2 * N], U8, name="wv_raw")
        x_scales = keep.tile([P, J], U8, name="x_scales", align_bytes=64)
        ws_raw = x_scales[:, HALF : HALF + N]
        x_rows = xT.rearrange("(p t) c -> p t c", t=PACK)
        st_rows = st.rearrange("(p t) j -> p t j", t=PACK)
        out_rows = out_0.rearrange("(p t) j -> p t j", t=PACK)
        out_words = out_1[0].rearrange("p j i -> p (j i)").bitcast(I32)

        def load_scales(n):
            q, first = n // 2, 4 * (n % 2)
            rows = wk_scales if first else wv_scales
            at = 32 * q + first
            nc.sync.dma_start(ws_raw[at : at + 4, :].bitcast(I32), rows[0, 4 * q : 4 * q + 4, :].bitcast(I32))

        nc.gpsimd.memset(ws_raw.bitcast(I32), 0)
        half_rows = wgt.rearrange("r (h c) -> (r h) c", h=2)[0 : 2 * P : GROUP + 1, :]
        nc.sync.dma_start(w_rows[:], half_rows.rearrange("u (v c) -> u v c", v=GROUP // 2))
        nc.sync.dma_start(offsets[:], offs)
        nc.sync.dma_start(planes[0][:], x_rows[:, 0, :])
        nc.sync.dma_start(planes[1][:], x_rows[:, 1, :])
        nc.sync.dma_start(wk_raw[:].bitcast(I32), wk_words[0].rearrange("p n i -> p (n i)").bitcast(I32))
        nc.sync.dma_start(planes[2][:], x_rows[:, 2, :])
        for n in range(EARLY_SCALES):
            load_scales(n)
        nc.sync.dma_start(planes[3][:], x_rows[:, 3, :])
        for n in range(EARLY_SCALES, 8):
            load_scales(n)
        nc.sync.dma_start(wv_raw[:].bitcast(I32), wv_words[0].bitcast(I32))
        state = {}
        for u in range(2):
            state[u] = keep.tile([P, PAIR, CHUNK], F32, name=f"state_unit{u}", align_bytes=64)[:]
            nc.sync.dma_start(state[u], st_rows[:, PAIR * u : PAIR * (u + 1), chunk_cols(0)])
        for c in range(1, CHUNKS):
            both = keep.tile([P, PACK, CHUNK], F32, name=f"state_chunk{c}")
            nc.sync.dma_start(both[:], st_rows[:, :, chunk_cols(c)])
            for u in range(2 * c, 2 * c + 2):
                state[u] = both[:, place(u)[1], place(u)[2]]

        w_turned = keep.tile([P, J // GROUP], F32, name="w_turned", align_bytes=64)
        w_spread = keep.tile([P, J], F32, name="w_spread", align_bytes=64)
        weight = keep.tile([P, J], F32, name="weight", align_bytes=64)
        halves = [slice(0, J // 2), slice(J // 2, J)]
        for b in range(2):
            square = slice(SQUARE * b, SQUARE * (b + 1))
            nc.vector.transpose(w_turned[:, square], w_rows[:, square])
        by_run = w_turned[:].rearrange("p (b h i) -> p i b h", b=2, h=2)
        parts = [chunk_cols(0), chunk_cols(1), halves[1]]
        for js in parts:
            runs = slice(js.start // (2 * SQUARE), js.stop // (2 * SQUARE))
            copy = nc.scalar.copy if js == halves[1] else nc.vector.tensor_copy
            copy(
                w_spread[:, js].rearrange("p (i b h r) -> p i b h r", b=2, h=2, r=GROUP),
                by_run[:, runs].unsqueeze(4).to_broadcast([P, runs.stop - runs.start, 2, 2, GROUP]),
            )
        for js in parts:
            nc.vector.transpose(weight[:, js], w_spread[:, js])

        wk = keep.tile([P, PACK, P], U32, name="wk", align_bytes=64)
        wv = keep.tile([P, PACK, P], U16, name="wv", align_bytes=64)
        ws = keep.tile([P, PACK, P], U8, name="ws", align_bytes=64)
        low = keep.tile([P, 2, J], F32, name="low")
        shared = keep.tile([P, 2 * J], F32, name="shared", align_bytes=64)
        high = shared[:].rearrange("p (t j) -> p t j", t=2)
        xg = [shared[:, 2 * J - 2 * CHUNK :].bitcast(BF16).rearrange("p (j t) -> p j t", t=PACK)]
        xg.extend(keep.tile([P, CHUNK, PACK], BF16, name=f"xg{c}", align_bytes=64)[:] for c in range(1, CHUNKS))
        x_codes = [keep.tile([P, CHUNK], I32, name=f"x_codes{c}", align_bytes=64) for c in range(2)]

        def deal(dealt, raw):
            nc.vector.tensor_copy(dealt.rearrange("p t m -> p m t"), raw.rearrange("p (m t) -> p m t", t=PACK))

        def gather(pair, t, js):
            picked = planes[t][:].indirect(offsets[:, js.start // GROUP : js.stop // GROUP])
            nc.vector.tensor_tensor(pair[:, t % 2, js], picked, weight[:, js], MULT)

        def weave_x(pair, first, c):
            nc.scalar.copy(xg[c][:, :, first : first + 2], pair[:, :, chunk_cols(c)].rearrange("p t j -> p j t"))

        def quantize_x(c):
            nc.vector.quantize_mx(
                out=x_codes[c][:].bitcast(FP8X4), scales=x_scales[:, chunk_cols(c)],
                in_=xg[c].rearrange("p j t -> p (j t)"),
            )

        for js in halves:
            gather(low, 0, js)
        for js in halves:
            gather(low, 1, js)
        nc.scalar.copy(wk[:].rearrange("p t m -> p m t"), wk_raw[:].rearrange("p (m t) -> p m t", t=PACK))
        for c in range(CHUNKS):
            weave_x(low, 0, c)
        gather(high, 2, slice(0, J))
        for js in (slice(0, HALF), slice(HALF, CHUNK)):
            gather(high, 3, js)
            nc.scalar.copy(xg[0][:, js, 2:4], high[:, :, js].rearrange("p t j -> p j t"))
        for n in range(2):
            deal(ws[:, :, n * P // 2 : (n + 1) * P // 2], ws_raw[:, n * N // 2 : (n + 1) * N // 2])
        gather(high, 3, chunk_cols(1))
        weave_x(high, 2, 1)
        quantize_x(0)
        deal(wv[:], wv_raw[:].bitcast(U16))
        for c in range(2, CHUNKS):
            gather(high, 3, chunk_cols(c))
            weave_x(high, 2, c)
        quantize_x(1)

        y = {c: keep.tile([P, PACK, CHUNK], F32, name=f"y{c}") for c in range(1, CHUNKS)}
        woven = keep.tile([P, J, PACK], BF16, name="woven", align_bytes=64)
        y_codes = keep.tile([P, J], I32, name="y_codes", align_bytes=64)
        y_scales = keep.tile([P, J], U8, name="y_scales", align_bytes=64)
        held = {u: keep.tile([P, PAIR, CHUNK], F32, name=f"held{u}")[:] for u in GPSIMD_PRODUCTS}
        ke, ve, gate = {}, {}, {}

        def shaped(tile, u):
            ts = place(u)[1]
            return tile[:].rearrange("p (t j) -> p t j", t=ts.stop - ts.start)

        def multiply(u, banks, name, words, packed, row):
            c, ts, cols = place(u)
            js = slice(c * CHUNK + cols.start, c * CHUNK + cols.stop)
            out = shaped(banks.tile([P, BANK], F32, name=name), u)
            for t in range(ts.start, ts.stop):
                nc.tensor.matmul_mx(
                    out=out[:, t - ts.start, :], lhsT=words[:, t, :].bitcast(packed), lhsT_scale=ws[row:P, t, :],
                    rhs=x_codes[c][:, cols].bitcast(FP8X4), rhs_scale=x_scales[:, js], start=True, stop=True,
                )
            return out

        def open_gate(u):
            logit = shaped(ring.tile([P, BANK], F32, name="logit"), u)
            gate[u] = shaped(ring.tile([P, BANK], F32, name="gate"), u)
            if u in GPSIMD_PRODUCTS:
                nc.scalar.copy(held[u], ve[u])
            nc.vector.tensor_tensor(logit, ke[u], state[u], MULT)
            nc.scalar.activation(gate[u], logit, TANH)

        def weave_y(c, n):
            cols = slice(n * HALF, (n + 1) * HALF)
            out = woven[:, c * CHUNK + cols.start : c * CHUNK + cols.stop, :]
            if (c, n) in GPSIMD_WEAVES:
                nc.gpsimd.tensor_scalar(out, y[c][:, :, cols].rearrange("p t j -> p j t"), 1.0, -0.0, MULT, ADD)
            else:
                copy = nc.vector.tensor_copy if (c, n) == (CHUNKS - 1, 1) else nc.scalar.copy
                copy(
                    out.rearrange("p (a i) t -> p a t i", i=4), y[c][:, :, cols].rearrange("p t (a i) -> p a t i", i=4)
                )

        def let_through(u):
            c, ts, cols = place(u)
            if u in GPSIMD_PRODUCTS:
                nc.gpsimd.tensor_tensor(y[c][:, ts, cols], held[u], gate[u], MULT)
            else:
                nc.vector.tensor_tensor(y[c][:, ts, cols], ve[u], gate[u], MULT)
            nc.sync.dma_start(
                out_rows[:, ts, c * CHUNK + cols.start : c * CHUNK + cols.stop], y[c][:, ts, cols]
            )
            if ts.stop == PACK:
                for n in range(cols.start // HALF, cols.stop // HALF):
                    if (c, n) != (CHUNKS - 1, 1):
                        weave_y(c, n)

        def quantize_y(js):
            nc.vector.quantize_mx(
                out=y_codes[:, js].bitcast(FP8X4), scales=y_scales[:, js],
                in_=woven[:, js, :].rearrange("p j t -> p (j t)"),
            )

        def store_words(js):
            nc.sync.dma_start(out_words[:, js], y_codes[:, js])

        ke[0] = multiply(0, key_banks, "ke", wk, FP8X4, 4)
        for u in range(UNITS):
            if u + 1 < UNITS:
                ke[u + 1] = multiply(u + 1, key_banks, "ke", wk, FP8X4, 4)
            ve[u] = multiply(u, value_banks, "ve", wv, FP4X4, 0)
            if u >= UNITS - 2:
                let_through(u - LAG)
            open_gate(u)
            if u == 1:
                for c in range(2, CHUNKS):
                    x_codes.append(
                        keep.tile([P, CHUNK], I32, name=f"x_codes{c}", tag=f"state_unit{c - 2}", align_bytes=64)
                    )
                    quantize_x(c)
                y[0] = keep.tile([P, PACK, CHUNK], F32, name="y0", tag=f"xg{CHUNKS - 1}", align_bytes=64)
            if LAG <= u < UNITS - 2:
                let_through(u - LAG)
        for u in range(UNITS - LAG, UNITS):
            let_through(u)
        quantize_y(halves[0])
        store_words(halves[0])
        weave_y(CHUNKS - 1, 1)
        quantize_y(chunk_cols(CHUNKS - 2))
        store_words(chunk_cols(CHUNKS - 2))
        quantize_y(chunk_cols(CHUNKS - 1))
        store_words(chunk_cols(CHUNKS - 1))
        for q in range(4):
            queue = nc.scalar if q // 2 else nc.sync
            queue.dma_start(
                out_2[0, 4 * q : 4 * q + 4, :].bitcast(I32), y_scales[32 * q : 32 * q + 4, :].bitcast(I32)
            )
